import numpy as np, ml_dtypes
CORES = [40,41,42,43,44,45,46,47]
N = 8
BF = ml_dtypes.bfloat16
def gentries(a):
    return np.ascontiguousarray(a.reshape(8, 16, -1).transpose(0, 2, 1)).reshape(8, -1)
def gtable(e):
    e = np.asarray(e); return np.ascontiguousarray(e.reshape(8, -1, 16).transpose(0, 2, 1)).reshape(128, -1).astype(np.int32)
B, J, CAP, RO, Q = 3072, 4096, 32, 4, 4096
LN, LJ = 3, 12
M = N * CAP; W = B + RO * M
WT = (14 * np.arange(16) + 9)[:, None]
def decode(n):
    C = np.add.accumulate((n * n[..., ::-1]) >> 12, axis=-1)
    x = (C[..., -1:] * np.arange(J)) >> LJ
    return np.add.reduce((C[..., None] <= x[..., None, :]).astype(np.int64), axis=-2)
def combine(x, y, z):
    q = x.shape[-1] // 4
    k = np.concatenate([np.minimum(x[..., :q], y[..., :q]), np.maximum(x[..., q:2 * q], y[..., q:2 * q]), np.abs(x[..., 2 * q:3 * q] - y[..., 2 * q:3 * q]), x[..., 3 * q:] + y[..., 3 * q:]], axis=-1)
    return np.minimum(k, z)
def sizes(c):
    c = np.sort(c, axis=-1); z = np.zeros(c.shape[:-1] + (1,), np.int64)
    return np.diff(np.concatenate([z, c, z + B - 256], axis=-1), axis=-1) + 64
def span(rng, v, share):
    o = rng.integers(0, B, (3, N, 8, 1, 2048)); x, y, z = [np.take_along_axis(v, i, 3) for i in o]
    s = np.sort(np.add.reduce(combine(x, y, z), axis=2), axis=-1)
    m = np.minimum(np.maximum((2048 * share).astype(np.int64), 1), 2048); k = (rng.random((N, 8)) * (2048 - m)).astype(np.int64)
    return np.concatenate([np.take_along_axis(s, k[..., None], 2), np.take_along_axis(s, (k + m - 1)[..., None], 2)], axis=2)
def shares(rng):
    return CAP * N * 2.0 ** -LJ * rng.choice(np.array([0.4, 0.8, 1.0, 1.5]), (N, 8))
def parts(rng):
    e = rng.choice(np.array([0.5, 1.0, 1.0, 2.0]), (N, 8, 16, 1))
    v = np.minimum((256 * rng.random((N, 8, 16, B)) ** e).astype(np.int64), 255)
    n = sizes(rng.integers(0, B - 255, (N, 8, 3))); r = rng.integers(0, 4096, (3, N, 8, RO, J))
    u = (rng.random((N, 8, Q)) < rng.choice(np.array([0.05, 0.2, 0.5]), (N, 8, 1))).astype(np.int64)
    return v, n, span(rng, v, shares(rng)), r, u
def pack(v, n, lim, r, u):
    t = [np.stack([gtable(a.reshape(8, -1)) for a in b]) for b in r]
    return {"bank": np.ascontiguousarray(v.reshape(N, 128, B)).astype(np.float32).astype(BF), "ncl": n.astype(np.int32), "lim": lim.astype(np.int32),
            "ra": t[0], "rb": t[1], "rc": t[2], "used": u.astype(np.int32)}
def goals(rng, k):
    return np.stack([rng.permutation(Q - 1)[:k] + 1 for p in range(N)]) * N + np.arange(N)[:, None]
def keyed(rng, d):
    c = rng.integers(1, 256, (16, d.size)); c[[0, 1, 15]] = rng.integers(40, 101, (3, d.size))
    e = (d - np.add.reduce(c * WT, axis=0)) & (N * Q - 1)
    c[15] += e // 219; e = e % 219; c[0] += e // 9 - 5 * (e % 9); c[1] += 2 * (e % 9)
    return c
def put(rng, v, n, q, g, d):
    s = np.add.accumulate(n[q, g]) - n[q, g]; v[q, g][:, s] = 255; v[q, g][:, s + 1] = 0
    w = rng.permutation(np.setdiff1d(np.arange(B), np.concatenate([s, s + 1])))[:d.size]
    v[q, g][:, w] = keyed(rng, d.reshape(-1)); return w.reshape(d.shape)
def deal(rng, col, at, w):
    o = rng.permutation(np.repeat(np.arange(N), CAP)); at = np.sort(rng.permutation(at)[:M])
    for p in range(N): col[at[o == p]] = w[p]
def play(r, n, q, g, t, col):
    h = J // 4; k = B + t * M; r[:2, q, g, t] = 0; r[2, q, g, t] = (col * 4096 + k - 1) // k
    if t == 0:
        m = n[q, g][3 - decode(n[q, g])[2 * h:3 * h]]; r[1, q, g, 0, 2 * h:3 * h] = (4096 + m - 1) // m
def setup_inputs(rng):
    return pack(*parts(rng))
def setup_inputs_room(rng):
    v, n, lim, r, u = parts(rng); lim[:] = (1500, 2600)
    for q in range(N):
        for g in range(8):
            m = n[q, g]; p = np.concatenate([np.arange(k) for k in m]); live = p >= np.repeat(m // 2, m)
            c = np.where(live, rng.integers(110, 150, (16, B)), rng.integers(0, 90, (16, B)))
            c[0] += (p - np.add.reduce(c * WT, axis=0)) & (N - 1)
            c[:, p == 0] = 0; c[:, p == 1] = 255; v[q, g] = c
            t = rng.choice(np.array([0, 1, CAP - 1, CAP, CAP + 1, 2 * CAP]), N)
            if q == 0: t[1] = (CAP, CAP + 1, CAP - 1, CAP, 0, 1, 2 * CAP, CAP)[g]
            if g == 6: t[2] = 0
            own = np.full(J, -1); own[rng.permutation(J)[:int(np.sum(t))]] = rng.permutation(np.repeat(np.arange(N), t))
            a = decode(m); na = m[a]; nb = m[3 - a]; h = na // 2
            dead = 2 + (rng.random(J) * (h - 2)).astype(np.int64)
            good = h + (own - h) % N + N * (rng.random(J) * ((na - h - N) // N + 1)).astype(np.int64)
            i = np.where(own < 0, dead, good); y = (np.arange(J) < J // 4).astype(np.int64)
            r[0, q, g, 0] = (i * 4096 + na - 1) // na; r[1, q, g, 0] = (y * 4096 + nb - 1) // nb; r[2, q, g, 0] = (4096 + B - 1) // B
    return pack(v, n, lim, r, u)
def setup_inputs_ends(rng):
    v, n, lim, r, u = parts(rng); v[..., 0] = 0; v[..., B - 1] = 255
    for g in range(4):
        n[:, g] = 64; n[:, g, g] = B - 192
    n[:, 5] = n[:, 2]; lim[0, 5] = (1, 4080)
    for g in (0, 2, 4): r[:, :, g] = rng.choice(np.array([0, 1, 4094, 4095]), (3, N, RO, J))
    lim[:, 0] = (0, 4080); lim[:, 2] = (4080, 4080); lim[:, 4] = (0, 0); lim[:, 6, 0] = lim[:, 6, 1]
    r[:, :, 2, 0, J - 1] = 4095; r[2, :, 4, 0, :8] = 0; u[:, 2] = 0; u[:, 4] = 0
    r[2, :, 0, 0, :8] = 0; u[:, 0] = 0
    lim[:, 1] = (1, 4080); lim[:, 3] = (1, 4080); lim[:, 7] = (0, 4079); u[:, 1] = 0; u[:, 3] = 0; u[:, 7] = 0
    full = goals(rng, RO * M).reshape(N, RO, N, CAP)
    grid = goals(rng, M).reshape(N, N, CAP); grid[1:, N - 1, CAP - 1] = grid[1:, 0, 0]
    many = goals(rng, 2 * CAP); at = np.concatenate([np.arange(J // 4, J // 2), np.arange(3 * J // 4, J)])
    for q in range(N):
        w = put(rng, v, n, q, 3, full[:, :, q])
        for t in range(RO):
            col = np.full(J, 1); deal(rng, col, at, w[:, t]); play(r, n, q, 3, t, col)
        i = J // 8 + rng.permutation(J // 8)[:4]; r[0, q, 3, RO - 1, i] = rng.integers(1000, 4096, 4); r[2, q, 3, RO - 1, i] = 0
        w = put(rng, v, n, q, 7, grid[:, q])
        if q == N - 1: w[0, CAP - 1] = 1
        col = np.zeros(J, np.int64); deal(rng, col, np.arange(J), w); play(r, n, q, 7, 0, col)
        w = put(rng, v, n, q, 1, many[(q + 1) % N]); col = np.full(J, 1); k = J // 4
        if q > 0: k += int(rng.integers(0, CAP))
        i = np.sort(rng.permutation(J // 2)[:k]); col[i] = w[rng.integers(0, CAP, k)]; col[i[:CAP]] = w[:CAP]
        col[J // 2 + rng.permutation(J // 2)[:2 * CAP]] = np.tile(w[CAP:], 2); play(r, n, q, 1, 0, col)
    return pack(v, n, lim, r, u)
def setup_inputs_alike(rng):
    v, n, lim, r, u = parts(rng)
    a = rng.integers(1, 255, (8, 16, 3)); tw = np.zeros((16, 1), np.int64); tw[:4, 0] = (1, -1, -1, 1)
    pool = np.concatenate([a, a + tw], axis=2)
    for g in range(1, 8, 2):
        v[:, g] = pool[g][:, rng.integers(0, 6, (N, B))].transpose(1, 0, 2)
        for q in range(N):
            e = np.add.accumulate(n[q, g]); v[q, g][:, e - n[q, g]] = pool[g][:, :1]; v[q, g][:, e - 1] = pool[g][:, 3:4]
    lim[:, 1::2] = (0, 4080); u[:, 1::2] = 0; r[:, :, 1::2, 0, 0] = 0; r[:, :, 1::2, 0, 1] = 4095
    v[:, 2] = v[0, 2]; n[:, 2] = n[0, 2]; lim[:, 2] = lim[0, 2]; r[:, :, 2] = r[:, :1, 2]
    return pack(v, n, lim, r, u)
def setup_inputs_cold(rng):
    v, n, lim, r, u = parts(rng); o = rng.permutation(N); g = int(rng.integers(0, 8))
    lim[o[0]] = (1, 0); lim[o[0], 1::2] = (1600, 1000); lim[o[1]] = (0, 4080)
    lim[:, g] = (1700, 1100); lim[o[0], g] = (2000, 1999); lim[o[1], g] = (4080, 0); u[:, (g + 1) % 8] = 1; u[:, (g + 2) % 8] = 0
    u[o[2], (g + 3) % 8] = 1
    return pack(v, n, lim, r, u)
def setup_inputs_spread(rng):
    v, n, lim, r, u = parts(rng)
    v = np.minimum((np.exp2(8 * rng.random((N, 8, 1, B))) * rng.random((N, 8, 16, B))).astype(np.int64), 255)
    n = sizes(((B - 256) * rng.random((N, 8, 3)) ** 4).astype(np.int64))
    e = rng.choice(np.array([0.5, 1.0, 2.0, 3.0]), (3, N, 8, RO, 1)); r = np.minimum((4096 * rng.random((3, N, 8, RO, J)) ** e).astype(np.int64), 4095)
    u = (rng.random((N, 8, Q)) < 0.8 * rng.random((N, 8, 1))).astype(np.int64)
    return pack(v, n, span(rng, v, shares(rng)), r, u)
def check_inputs(d):
    bad = []; b = np.asarray(d["bank"]).astype(np.float32)
    if not np.all((b >= 0) & (b <= 255) & (b == np.floor(b))): bad.append("bank: whole numbers from 0 to 255")
    for k, lo, hi in (("ncl", 64, B), ("lim", 0, 4080), ("ra", 0, 4095), ("rb", 0, 4095), ("rc", 0, 4095), ("used", 0, 1)):
        if np.min(d[k]) < lo or np.max(d[k]) > hi: bad.append("range of " + k)
    if np.any(np.sum(np.asarray(d["ncl"]).astype(np.int64), axis=-1) != B): bad.append("sums of ncl")
    return bad
def reference(bank, ncl, lim, ra, rb, rc, used):
    v = np.zeros((N, 8, 16, W), np.int32); v[..., :B] = bank.astype(np.float32).astype(np.int32).reshape(N, 8, 16, B)
    n = np.zeros((N, 8, 4 + RO), np.int64); n[:, :, :4] = ncl
    la, lb, lc = [np.stack([gentries(a) for a in b]).astype(np.int64).reshape(N, 8, RO, J) for b in (ra, rb, rc)]
    free = used == 0; lo = lim[:, :, :1]; hi = lim[:, :, 1:]; take = np.take_along_axis
    for t in range(RO):
        s = 4 + t; m = n[:, :, :s].copy(); start = np.add.accumulate(m, axis=2) - m; tot = np.add.reduce(m, axis=2)
        a = decode(m); b = s - 1 - a
        ix = take(start, a, 2) + ((take(m, a, 2) * la[:, :, t]) >> 12)
        iy = take(start, b, 2) + ((take(m, b, 2) * lb[:, :, t]) >> 12)
        iz = (tot[:, :, None] * lc[:, :, t]) >> 12
        x, y, z = [take(v, i[:, :, None, :], 3) for i in (ix, iy, iz)]
        k = combine(x, y, z)
        total = np.add.reduce(k, axis=2); key = np.add.reduce(k * WT, axis=2)
        alive = (total >= lo) & (total <= hi); owner = key & (N - 1); bucket = (key >> LN) & (Q - 1)
        for p in range(N):
            for g in range(8):
                got = [np.flatnonzero(alive[q, g] & (owner[q, g] == p))[:CAP] for q in range(N)]
                c = np.concatenate([k[q, g][:, got[q]] for q in range(N)], axis=1); bu = np.concatenate([bucket[q, g, got[q]] for q in range(N)])
                first = np.sort(np.unique(bu, return_index=True)[1])
                keep = first[free[p, g, bu[first]]]; e = int(tot[p, g])
                v[p, g][:, e:e + len(keep)] = c[:, keep]; free[p, g, bu[keep]] = False; n[p, g, s] = len(keep)
    return {"y": np.ascontiguousarray(v[..., B:]).reshape(N, 128, RO * M).astype(np.float32).astype(BF)}

@@ -1,0 +1,467 @@
+from concourse.bass import DstId, RemoteDMATransfer
+from concourse.mybir import dt, AluOpType as ALU, AxisListType as AX, ActivationFunctionType as AF
+
+B, J, CAP, RO, NR = 3072, 4096, 32, 4, 8
+M1 = 1.5 * 2.0 ** 23
+MN = 1.5 * 2.0 ** 16
+M32 = 1.5 * 2.0 ** 28
+M4096 = 1.5 * 2.0 ** 35
+MID = 1920
+SEG = 41
+f32, bf, i32, u16, f16 = "float32", "bfloat16", "int32", "uint16", "float16"
+
+SCRATCH = {}
+for _d, _l in (
+    (bf, "bankS 4352,K 4112,YG 4096,FX 4096,XG 4096,ONE 256,ZERO 256,TRI 128,BID 128,DG 128,NDG 128,WCP 16,W0C 8,WBL 128,BON 128,W0 128,LI 2048,LP 2048,"
+         "COLT 256,CL 128,DM 16 16,RS 512,RSS 144,MSK 144,MI 256,JC 1,RH 256,LQ 1024,OWN 256,O 2048,S4 256,U 2048,Z 328,EO 512,CU 512,IN 512,C2 512,SMM 144,SS 144,UG 256,"
+         "E3 16 272,KP 256,POS 256,X 256,send 1024,land 1024"),
+    (i32, "USED 4368,RA 1024,RB 1024,RC 1024,PID 1,TI 8,ONEI 256,OI 256,OJ 256,KLI 16,KLJ 16"),
+    (f32, "CC 32,IR 256,IG 128,II 128,GB 256,I16 16 16,IF 256,I9 144,JL 16,ONEF 128,MK 8,MD 8,MS 8,MQ 128,RQ 32,NEGM 8,IT 128,MIDT 256,HALF 256,F4 32,R8 8,TC 8,PP 8,PR 8,"
+          "SEL 16,SM 8,CS 16,DQ 32,DS 32,HI 4,LO 4,CIT 128,W1 256,V1 256,Z1 256,J16 16,R32 16,INV 16,BL 16,ZT 16,WJ 16,D1 16,UJ 16,E1 16"),
+    (u16, "OX 256,OY 256,OZ 256,OFJ 16,BU 16,DU 16,EU 16,OC 16"),
+    (f16, "RP 8,LJ 256,KBH 256"),
+):
+    for _x in _l.split(","):
+        _x = _x.split()
+        SCRATCH[_x[0]] = ("sbuf", [128] + [int(v) for v in _x[1:]], _d)
+SCRATCH.update({"NL": ("sbuf", [8, 4], i32), "LM": ("sbuf", [8, 2], i32), "NLF": ("sbuf", [8, 4], f32), "LMF": ("sbuf", [8, 8], f32),
+                "SL8": ("sbuf", [8, 128], f32), "DM8": ("sbuf", [8, 512], f32)})
+for _k in range(8):
+    SCRATCH["b%d" % _k] = ("psum", [128, 512], f32)
+_DMAS = ["ncl", "lim", "bank", "ra0", "rb0", "rc0", "ra1", "rb1", "rc1", "used", "out"]
+SEMAPHORES = ["sV", "sA", "sP", "sG"] + ["d_" + n for n in _DMAS] + ["arr%d" % t for t in range(RO)] + ["sent%d" % t for t in range(RO)]
+BANKS = tuple("b%d" % k for k in range(8))
+
+
+def rank_program(g, core, T, topo):
+    rank = T.rank_of(core)
+    if rank is None:
+        return
+    eng = {"V": g.vector, "A": g.scalar, "P": g.tensor, "G": g, "S": g.sync}
+    cnt = {"V": 0, "A": 0, "P": 0, "G": 0}
+    seen = {e: {} for e in eng}
+    lastw, readers = {}, {}
+
+    def wait(e, sem, val):
+        if seen[e].get(sem, 0) < val:
+            eng[e].wait_ge(T.sem[sem], val)
+            seen[e][sem] = val
+
+    def order(e, r, w):
+        req = {}
+        me = "s" + e
+
+        def add(ev):
+            if ev is not None:
+                req[ev[0]] = max(req.get(ev[0], 0), ev[1])
+        for k in r:
+            add(lastw.get(k))
+        for k in list(w) + [k for k in r if k in BANKS]:
+            add(lastw.get(k))
+            for ev in readers.get(k, {}).items():
+                if ev[0] != me:
+                    add(ev)
+        if e == "P":
+            req.pop("sP", None)
+        for sem in sorted(req):
+            wait(e, sem, req[sem])
+
+    def note(ev, r, w):
+        for k in r:
+            readers.setdefault(k, {})[ev[0]] = ev[1]
+        for k in w:
+            lastw[k] = ev
+            readers[k] = {}
+
+    def do(e, call, r, w):
+        r, w = r.split(), w.split()
+        order(e, r, w)
+        cnt[e] += 1
+        call(eng[e]).then_inc(T.sem["s" + e], 1)
+        note(("s" + e, cnt[e]), r, w)
+
+    def dma(e, name, out, in_, r, w):
+        r, w = r.split(), w.split()
+        order(e, r, w)
+        eng[e].dma_start(out, in_).then_inc(T.sem["d_" + name], 16)
+        note(("d_" + name, 16), r, w)
+
+    def ts(out, in0, s1, op0, r, w, s2=None, op1=None):
+        if op1 is None:
+            do("V", lambda v: v.tensor_scalar(out, in0, s1, None, op0), r, w)
+        else:
+            do("V", lambda v: v.tensor_scalar(out, in0, s1, s2, op0, op1), r, w)
+
+    def tt(out, a, b, op, r, w):
+        do("V", lambda v: v.tensor_tensor(out, a, b, op), r, w)
+
+    def cp(out, a, r, w):
+        do("V", lambda v: v.tensor_copy(out, a), r, w)
+
+    def ms(ap, c, w):
+        do("V", lambda v: v.memset(ap, c), "", w)
+
+    def mm(out, l, rh, r, w, start=True, stop=True):
+        do("P", lambda p: p.matmul(out, l, rh, start, stop), r, w)
+
+    def act(out, a, fn, r, w, scale=1.0, bias=0.0):
+        do("A", lambda s: s.activation(out, a, fn, bias=bias, scale=scale), r, w)
+
+    def iota(ap, pat, cm, w, base=0):
+        do("G", lambda q: q.iota(ap, pat, base, cm, allow_small_or_imprecise_dtypes=True), "", w)
+
+    def scan(out, d0, d1, op0, op1, r, w):
+        do("V", lambda v: v.tensor_tensor_scan(out, d0, d1, 0.0, op0, op1), r, w)
+
+    dma("S", "ncl", T.NL[:, :], T.ncl[:, :], "", "NL")
+    dma("S", "lim", T.LM[:, :], T.lim[:, :], "", "LM")
+    dma("A", "rb0", T.RB[:, 0:256], T.rb[:, 0:256], "", "RB0")
+    dma("A", "ra0", T.RA[:, 0:256], T.ra[:, 0:256], "", "RA0")
+    dma("A", "rc0", T.RC[:, 0:256], T.rc[:, 0:256], "", "RC0")
+    dma("S", "bank", T.bankS[:, 0:B], T.bank[:, :], "", "bk")
+    iota(T.PID[:, :], [[1, 1]], 1, "PID")
+    iota(T.IG[:, :], [[1, 8], [0, 16]], 0, "IG")
+    iota(T.II[:, :], [[0, 8], [1, 16]], 0, "II")
+    iota(T.IR[:, :], [[1, 256]], 0, "IR")
+    ms(T.ONE[:, :], 1.0, "ONE")
+    for n in ("b", "a", "c"):
+        dma("S", "r%s1" % n, T["R" + n.upper()][:, 256:1024], T["r" + n][:, 256:1024], "", "R%s1" % n.upper())
+    do("G", lambda q: q.affine_select(T.DG[:, :], T.ONE[:, 0:128], [[1, 128]], ALU.is_equal, 0.0, 0, -1), "ONE", "DG")
+    iota(T.bankS[:, B:4096], [[0, 1024]], 0, "bkz")
+    iota(T.GB[:, :], [[1, 8], [0, 32]], 0, "GB")
+    do("G", lambda q: q.affine_select(T.TRI[:, :], T.ONE[:, 0:128], [[1, 128]], ALU.is_gt, 0.0, 0, -1), "ONE", "TRI")
+    do("G", lambda q: q.affine_select(T.BID[:, :], T.DG[:, :], [[1, 128]], ALU.not_equal, -1.0, -1, -1), "DG", "BID")
+    iota(T.IF[:, :], [[0, 16], [1, 16]], 0, "IF")
+    iota(T.I9[:, :], [[0, 16], [1, 9]], 0, "I9")
+    iota(T.I16[:, :, :], [[0, 16], [1, 16]], 0, "I16")
+    iota(T.JL[:, :], [[16, 16]], 0, "JL")
+    iota(T.LI[:, :], [[0, 2048]], 0, "LI")
+    iota(T.LP[:, :], [[0, 2048]], 0, "LP")
+    iota(T.USED[:, 0:4096], [[0, 4096]], 0, "USED")
+    iota(T.USED[:, 4096:4112], [[0, 16]], 0, "USEDx", 1)
+    iota(T.ONEI[:, :], [[0, 256]], 0, "ONEI", 1)
+    dma("S", "used", T.USED[0:128:16, 0:4096], T.used[:, :], "", "USED")
+
+    CC = T.CC
+    col = {n: CC[:, k:k + 1] for k, n in enumerate(
+        ["pid", "i", "m", "typ", "grp", "p8", "c16", "wt", "podd", "sgs", "msg", "off", "tm1", "cval", "i0",
+         "mm1", "sm0", "sm1", "sm2", "sm3", "t0", "t1", "c32"])}
+    for k, (sh, an) in enumerate([(0, 255), (0, 15), (1, 7), (0, 1), (4, 7), (0, 7), (3, 15)]):
+        ts(T.TI[:, k:k + 1], T.PID[:, :], sh, ALU.arith_shift_right, "PID", "TI%d" % k, an, ALU.bitwise_and)
+    cp(CC[:, 0:7], T.TI[:, 0:7], "TI0 TI1 TI2 TI3 TI4 TI5 TI6", "CC")
+    for n, src, a, b, key in (("tm1", "typ", 1.0, -1.0, "CCt"), ("sm0", "m", -1.0, 3.0, "CCx0"), ("mm1", "m", 1.0, -1.0, "CCn"), ("msg", "typ", -2.0, 1.0, "CCm"),
+                              ("off", "typ", -1.0, 1.0, "CCf"), ("wt", "i", 14.0, 9.0, "CCw"), ("sm1", "m", -1.0, 4.0, "CCx1"), ("sm2", "m", -1.0, 5.0, "CCx2"),
+                              ("sm3", "m", -1.0, 6.0, "CCx3"), ("podd", "p8", 2.0, 1.0, "CCo"), ("c32", "c16", 1.0, 16.0, "CC2")):
+        act(col[n], col[src], AF.Copy, "CC", key, a, b)
+        if n == "mm1":
+            act(T.COLT[:, :], T.IR[:, :], AF.Identity, "IR CCt", "COLT", 1.0, col["tm1"])
+    act(T.JC[:, :], col["pid"], AF.Copy, "CC", "JC")
+    ts(col["sgs"], col["typ"], 2.0 / 4096, ALU.mult, "CC", "CCs", -1.0 / 4096, ALU.add)
+    ts(T.BON[:, :], T.IG[:, :], col["grp"], ALU.is_equal, "IG CC", "BON")
+    ts(T.SL8[:, :], T.IG[0:8, :], CC[0:8, 0:1], ALU.is_equal, "IG CC", "SL8")
+    ts(T.IT[:, :], T.II[:, :], col["sgs"], ALU.mult, "II CCs", "IT", 9999.0 / 4096, ALU.add)
+    ts(T.MK[:, :], T.IR[:, 0:8], col["m"], ALU.is_equal, "IR CC", "MK")
+    ts(col["i0"], col["i"], 0.0, ALU.is_equal, "CC", "CCi")
+    tt(T.IT[:, :], T.IT[:, :], T.BON[:, :], ALU.mult, "IT BON", "IT")
+    ts(T.MS[:, :], T.IR[:, 0:8], col["mm1"], ALU.is_equal, "IR CCn", "MS")
+    ms(T.RQ[:, :], 1.0, "RQ")
+    ts(T.IT[:, :], T.IT[:, :], -9999.0 / 4096, ALU.add, "IT", "IT")
+    ms(T.RQ[:, 0:32:8], 0.0, "RQ")
+    tt(T.MD[:, :], T.MK[:, :], T.MS[:, :], ALU.subtract, "MK MS", "MD")
+    cp(T.NLF[:, :], T.NL[:, :], "NL", "NLF")
+    for b in ("b0", "b7"):
+        mm(T[b][:, 0:4], T.SL8[:, :], T.NLF[:, :], "SL8 NLF", b)
+
+    def masks(t):
+        q, s = 32 * t, 4 + t
+        ts(T.PR[:, :], T.IR[:, 0:8], col["sm%d" % t], ALU.is_equal, "IR CCx%d" % t, "PR")
+        ts(T.DS[:, 0:8], T.IR[:, 0:8], 1.0, ALU.subtract, "IR CCx%d" % t, "DS", col["sm%d" % t], ALU.is_equal)
+        ts(T.DS[:, 24:32], T.IR[:, 0:8], float(s - 1), ALU.is_le, "IR", "DSd")
+        ts(T.MQ[:, q:q + 8], T.MD[:, :], 1.0 / 4096, ALU.mult, "MD", "MQ%d" % t)
+        tt(T.DS[:, 8:16], T.PR[:, :], T.DS[:, 0:8], ALU.subtract, "PR DS", "DSb")
+        ts(T.DQ[:, 0:8], T.DS[:, 24:32], T.MK[:, 0:1], ALU.mult, "DSd MK", "DQ")
+        cp(T.MQ[:, q + 16:q + 24], T.MS[:, :], "MS", "MQ%da" % t)
+        ts(T.MQ[:, q + 8:q + 16], T.DS[:, 8:16], 1.0 / 4096, ALU.mult, "DSb", "MQ%db" % t)
+        tt(T.MQ[:, q + 24:q + 32], T.DQ[:, 0:8], T.PR[:, :], ALU.subtract, "DQ PR", "MQ%dc" % t)
+    masks(0)
+    ms(T.F4[:, :], 0.0, "F4")
+    ms(T.R8[:, :], 0.0, "R8")
+    ms(T.SEL[:, :], 0.0, "SEL")
+    for k in range(4):
+        cp(T.F4[:, 8 * k:8 * k + 4], T.b0[:, 0:4], "b0 F4", "F4%d" % k)
+        act(T.R8[:, 7 - k:8 - k], T.b7[:, k:k + 1], AF.Copy, "b7 R8", "R8%d" % k)
+    ms(T.NEGM[:, :], -M4096, "NEGM")
+    ts(col["t0"], col["i"], 1.0, ALU.is_equal, "CC", "CC0", 2.0 ** -13, ALU.mult)
+    ts(col["t1"], col["i"], 2.0, ALU.is_equal, "CC", "CC1", -float(MID), ALU.mult)
+    ms(T.TC[:, 0:1], float(B), "TC")
+    ts(col["cval"], col["i0"], -0.5, ALU.mult, "CCi CC0", "CCv", col["t0"], ALU.add)
+    ms(T.TC[:, 1:2], B / 4096.0, "TC1")
+    tt(col["cval"], col["cval"], col["t1"], ALU.add, "CCv CC1", "CCv")
+
+    bankk = "bk bkz"
+    c0 = -(MID + 0.5) + 2.0 ** -13
+    F4k, R8k = "F4 F40 F41 F42 F43", "R8 R80 R81 R82 R83"
+
+    def prep(t):
+        s = 4 + t
+        CS, SEL = T.CS, T.SEL
+        ct = SEL[:, s:s + 1]
+        c = slice(256 * t, 256 * t + 256)
+        tt(T.PP[:, 0:s], T.F4[:, 0:s], T.R8[:, 8 - s:8], ALU.mult, F4k + " " + R8k, "PP")
+        tt(T.DQ[:, :], T.F4[:, :], T.MQ[:, 32 * t:32 * t + 32], ALU.mult, F4k + " MQ%d MQ%da MQ%db MQ%dc" % (t, t, t, t), "DQ")
+        ts(T.PR[:, 0:s], T.PP[:, 0:s], -2047.5, ALU.add, "PP", "PR", M4096, ALU.add)
+        scan(T.DS[:, :], T.RQ[:, :], T.DQ[:, :], ALU.mult, ALU.add, "RQ DQ", "DS")
+        scan(SEL[:, 1:s + 1], T.PR[:, 0:s], T.NEGM[:, 0:s], ALU.add, ALU.add, "PR NEGM", "SEL")
+        ts(T.HI[:, 0:2], T.DS[:, 7:16:8], MN, ALU.add, "DS", "HI", MN, ALU.subtract)
+        ts(CS[:, 0:1], ct, 1.0 / 256, ALU.mult, "SEL", "CS0")
+        tt(T.SM[:, :], SEL[:, 0:8], T.MK[:, :], ALU.mult, "SEL MK", "SM")
+        do("V", lambda v: v.reciprocal(CS[:, 1:2], CS[:, 0:1]), "CS0", "CS1")
+        do("V", lambda v: v.tensor_reduce(CS[:, 2:3], T.SM[:, :], AX.X, ALU.add), "SM", "CS2")
+        ts(T.HI[:, 2:4], T.DS[:, 23:32:8], M32, ALU.add, "DS", "HI2", M32, ALU.subtract)
+        ts(CS[:, 3:4], CS[:, 2:3], CS[:, 1:2], ALU.mult, "CS1 CS2", "CS3", -0.46875, ALU.add)
+        tt(T.LO[:, :], T.DS[:, 7:32:8], T.HI[:, :], ALU.subtract, "DS HI HI2", "LO")
+        ts(CS[:, 4:5], CS[:, 3:4], M1, ALU.add, "CS3", "CS4", M1, ALU.subtract)
+        ts(T.Z1[:, :], T.RC[:, c], T.TC[:, 1:2], ALU.mult, "RC%d TC1" % (t > 0), "Z1", c0, ALU.add)
+        ts(CS[:, 5:6], CS[:, 4:5], CS[:, 0:1], ALU.mult, "CS0 CS2 CS4", "CS5", CS[:, 2:3], ALU.subtract)
+        ts(T.OZ[:, :], T.Z1[:, :], M1, ALU.add, "Z1", "OZ", M1 - MID, ALU.subtract)
+        ts(CS[:, 6:7], CS[:, 5:6], col["msg"], ALU.mult, "CS5 CCm CCf", "CS6", col["off"], ALU.add)
+
+    def lists(t):
+        CS, ct, k = T.CS, T.SEL[:, 4 + t:5 + t], "%d" % (t > 0)
+        c = slice(256 * t, 256 * t + 256)
+        ts(T.CIT[:, :], T.IT[:, :], ct, ALU.mult, "IT SEL", "CIT")
+        ts(T.RH[:, :], T.COLT[:, :], CS[:, 4:5], ALU.is_ge, "COLT CS4", "RH")
+        for b in ("b2", "b4"):
+            mm(T[b][:, 0:256], T.CL[:, :], T.ONE[:, :], "CL ONE", b, True, False)
+        for q, b in ((1, "b1"), (3, "b2"), (0, "b3"), (2, "b4")):
+            for h, src in ((0, "HI"), (1, "LO")):
+                n = 2 * q + h
+                ts(T.LQ[:, 128 * n:128 * n + 128], T.CIT[:, :], CS[:, 6:7], ALU.is_ge, "CIT CS6 HI HI2 LO", "LQ%d" % n, T[src][:, q:q + 1], ALU.mult)
+                mm(T[b][:, 0:256], T.LQ[:, 128 * n:128 * n + 128], T.RH[:, :], "LQ%d RH" % n, b, q < 2 and h == 0, h == 1)
+        for w, r, o, bn, bs in (("V1", "RB", "OY", "b1", "b2"), ("W1", "RA", "OX", "b3", "b4")):
+            tt(T[w][:, :], T[bn][:, 0:256], T[r][:, c], ALU.mult, bn + " " + r + k, w)
+            tt(T[w][:, :], T[w][:, :], T[bs][:, 0:256], ALU.add, w + " " + bs, w)
+            ts(T[o][:, :], T[w][:, :], M1, ALU.add, w, o, M1 - MID, ALU.subtract)
+
+    win = T.bankS[:, 0:4096]
+
+    def build(t, h0, h1):
+        def y(q, dst="YG", lst="OY", a=0, n=1024):
+            o = 1024 * q + a
+            act(T[dst][:, o:o + n], win.indirect(T[lst][:, o // 16:(o + n) // 16]), AF.Copy, lst + " " + bankk, "%s%d%d" % (dst, q, a))
+
+        def x(q, a=0):
+            o = slice(1024 * q + a, 1024 * q + 1024)
+            tt(T.FX[:, o], win.indirect(T.OX[:, 64 * q + a // 16:64 * q + 64]), T.YG[:, o], (ALU.min, ALU.max, None, ALU.add)[q], "OX YG%d%d " % (q, a) + bankk, "FX%d%d" % (q, a))
+
+        def both(q, b, o, lh):
+            mm(T[b][:, :], T.DG[:, :], T.XG[:, o:o + 512], "DG XG%d0" % q, b, True, False)
+            mm(T[b][:, :], T[lh][:, :], T.YG[:, o:o + 512], "%s YG%d0" % (lh, q), b, False, True)
+
+        def z(q, a=0, n=1024):
+            o = 1024 * q + a
+            tt(T.K[:, o:o + n], win.indirect(T.OZ[:, o // 16:(o + n) // 16]), T.FX[:, o:o + n], ALU.min, "OZ FX%d%d FX%d512 " % (q, a, q) + bankk, "K%d%d" % (q, a))
+
+        def sums(q):
+            for b in range(32):
+                mm(T.b0[32 * q:32 * q + 32, b:512:32], T.K[:, 1024 * q + b:1024 * q + 1024:32], T.WCP[:, :], "WCP K%d0 K%d512" % (q, q), "b0")
+        y(0)
+        y(1)
+        h0()
+        x(0)
+        h1()
+        y(2)
+        y(2, "XG", "OX")
+        z(0)
+        both(2, "b5", 2048, "NDG")
+        both(2, "b6", 2560, "NDG")
+        sums(0)
+        x(1)
+        y(3, a=512, n=512)
+        y(3, n=512)
+        y(3, "XG", "OX", n=512)
+        both(3, "b7", 3072, "DG")
+        act(T.FX[:, 2048:2560], T.b5[:, :], AF.Abs, "b5", "FX20")
+        act(T.FX[:, 2560:3072], T.b6[:, :], AF.Abs, "b6", "FX2512")
+        act(T.FX[:, 3072:3584], T.b7[:, :], AF.Copy, "b7", "FX30")
+        z(1)
+        sums(1)
+        x(3, 512)
+        z(3, 512, 512)
+        z(2)
+        sums(2)
+        z(3, 0, 512)
+        sums(3)
+
+    def pick(t, h):
+        tt(T.Z1[:, :], T.b0[:, 0:256], T.MIDT[:, :], ALU.subtract, "b0 MIDT", "Z1")
+        act(T.b7[:, 0:256], T.Z1[:, :], AF.Abs, "Z1", "b7")
+        ts(T.OI[:, :], T.b0[:, 256:512], 2.0, ALU.mult, "b0", "OI", 1.0, ALU.add)
+        ts(T.OJ[:, :], T.OI[:, :], 15, ALU.bitwise_and, "OI", "OJ")
+        tt(T.b7[:, 256:512], T.b7[:, 0:256], T.HALF[:, :], ALU.is_le, "b7 HALF", "b7")
+        tt(T.OWN[:, :], T.OJ[:, :], T.b7[:, 256:512], ALU.mult, "OJ b7", "OWN")
+        for p in range(8):
+            ts(T.O[:, 256 * p:256 * p + 256], T.OWN[:, :], 2.0 * p + 1, ALU.is_equal, "OWN", "O%d" % p)
+        h()
+        for q in range(8):
+            mm(T.b6[:, SEG * q + 9:SEG * q + SEG], T.BID[:, :], T.OWN[:, 32 * q:32 * q + 32], "BID OWN", "b6")
+            mm(T.b6[:, SEG * q + 8:SEG * q + 9], T.BID[:, :], T.JC[:, :], "BID JC", "b6")
+        for b in range(32):
+            mm(T.b5[:, 0:64], T.TRI[:, :], T.O[:, b:2048:32], "TRI O0 O1 O2 O3 O4 O5 O6 O7", "b5", b == 0, b == 31)
+        for r in range(4):
+            ts(T.S4[:, 64 * r:64 * r + 64], T.b5[:, 0:64], -float(r), ALU.add, "b5", "S4%d" % r, 100.0, ALU.min)
+        for q in range(8):
+            mm(T.b6[:, SEG * q:SEG * q + 8], T.BID[:, :], T.S4[:, q:64:8], "BID S40", "b6")
+        act(T.Z[:, :], T.b6[:, 0:8 * SEG], AF.Copy, "b6", "Z")
+        for c in range(8):
+            ts(T.U[:, 256 * c:256 * c + 256], T.S4[:, :], 4.0 * c, ALU.is_le, "S40 S41 S42 S43", "U%d" % c)
+        for ch in (0, 1):
+            for lo, hi, b in ((9, SEG, "b%d" % (1 + ch)), (0, 9, "b%d" % (3 + ch))):
+                for q in range(8):
+                    mm(T[b][:, (hi - lo) * q:(hi - lo) * (q + 1)], T.U[:, 1024 * ch + q:1024 * ch + 1024:8], T.Z[:, SEG * q + lo:SEG * q + hi],
+                       "Z U%d U%d U%d U%d" % tuple(range(4 * ch, 4 * ch + 4)), b)
+        for ch in (0, 1):
+            d, b = slice(72 * ch, 72 * ch + 72), T["b%d" % (3 + ch)]
+            ts(T.EO[:, 256 * ch:256 * ch + 256], T["b%d" % (1 + ch)][:, 0:256], col["podd"], ALU.is_equal, "b%d CCo" % (1 + ch), "EO%d" % ch)
+            tt(T.SMM[:, d], b[:, 0:72], T.MSK[:, d], ALU.mult, "b%d MSK" % (3 + ch), "SMM%d" % ch)
+            ts(T.R32[:, 8 * ch:8 * ch + 8], b[:, 8:72:9], 32.0, ALU.mult, "b%d" % (3 + ch), "R32%d" % ch, -2048.0, ALU.add)
+        scan(T.SS[:, :], T.RSS[:, :], T.SMM[:, :], ALU.mult, ALU.add, "RSS SMM0 SMM1", "SS")
+        tt(T.EO[:, 0:512:32], T.EO[:, 0:512:32], T.SS[:, 8:144:9], ALU.add, "SS EO0 EO1", "EO0 EO1")
+        scan(T.CU[:, :], T.RS[:, :], T.EO[:, :], ALU.mult, ALU.add, "RS EO0 EO1", "CU")
+        ts(T.IN[:, 0:256], T.CU[:, 0:256], col["c16"], ALU.is_le, "CU CC", "IN0")
+        ts(T.IN[:, 256:512], T.CU[:, 256:512], col["c32"], ALU.is_le, "CU CC2", "IN1")
+        scan(T.C2[:, :], T.RS[:, :], T.IN[:, :], ALU.mult, ALU.add, "RS IN0 IN1", "C2")
+        tt(T.J16[:, :], T.C2[:, 31:512:32], T.R32[:, :], ALU.add, "C2 R320 R321", "J16")
+        do("V", lambda v: v.tensor_tensor(T.LJ[:, :], T.J16[:, :].indirect(T.OC[:, :]), T.MI[:, :], ALU.mult), "J16 OC MI", "LJ")
+        for ch in (0, 1):
+            mm(T.b5[:, ch:16:2], T.LJ[:, 128 * ch:128 * ch + 128], T.RP[:, :], "LJ RP", "b5")
+        ts(T.OFJ[:, :], T.b5[:, 0:16], 2048.0, ALU.add, "b5", "OFJ")
+        o = 256 * t
+        do("V", lambda v: v.tensor_copy(T.send[:, o:o + 256], T.K[:, 0:4112].indirect(T.OFJ[:, :])), "OFJ K00 K10 K20 K30 K3512 kinv", "snd%d" % t)
+        tr, k = [], 0
+        for p in range(NR):
+            if p == rank:
+                continue
+            dst = T.cores[p]
+            e = topo.engines(core, dst)
+            rid, pid, _se = topo.addr(dst)
+            tr.append(RemoteDMATransfer(dst_ids=[DstId(rid=rid, pnc=pid)], dma_engine_mask=(1 << e[2 * k]) | (1 << e[2 * k + 1]), remote_sem=T.sem["arr%d" % t],
+                                        srcs=[T.send[:, o + 32 * p:o + 32 * p + 32]], dsts=[T.land[:, o + 32 * rank:o + 32 * rank + 32]]))
+            k += 1
+        order("G", ["snd%d" % t], [])
+        g.remote_dma_fused(tr, local_sem=T.sem["sent%d" % t])
+        cp(T.land[:, o + 32 * rank:o + 32 * rank + 32], T.send[:, o + 32 * rank:o + 32 * rank + 32], "snd%d" % t, "lnd%d" % t)
+
+    def keep(t):
+        s, last = 4 + t, t == RO - 1
+        o, lk = 256 * t, "lnd%d" % t
+        lnd = T.land[:, o:o + 256]
+        wait("P", "arr%d" % t, 14)
+        mm(T.b3[:, 0:256], T.WBL[:, :], lnd, "WBL " + lk, "b3")
+        for i in range(16):
+            mm(T.b4[:, 0:16], T.LI[:, 128 * i:128 * i + 128], T.land[:, o + i:o + 256:16], "LI LI%d " % i + lk, "b4", i == 0, i == 15)
+        cp(T.OI[:, :], T.b3[:, 0:256], "b3", "OI")
+        ts(T.OJ[:, :], T.OI[:, :], 3, ALU.arith_shift_right, "OI", "OJ", 4095, ALU.bitwise_and)
+        ts(T.KBH[:, :], T.OJ[:, :], -2048.0, ALU.add, "OJ", "KBH")
+        cp(T.KLI[:, :], T.b4[:, 0:16], "b4", "KLI")
+        ts(T.INV[:, :], T.b4[:, 0:16], 0.0, ALU.is_lt, "b4", "INV", 4096.0, ALU.mult)
+        ts(T.KLJ[:, :], T.KLI[:, :], 3, ALU.arith_shift_right, "KLI", "KLJ", 4095, ALU.bitwise_and)
+        tt(T.BL[:, :], T.KLJ[:, :], T.INV[:, :], ALU.max, "KLJ INV", "BL")
+        cp(T.BU[:, :], T.BL[:, :], "BL", "BU")
+        do("V", lambda v: v.tensor_copy(T.UG[:, :], T.USED[:, 0:4112].indirect(T.BU[:, :])), "USED USEDx BU", "UG")
+        mm(T.b6[:, 0:256], T.W0[:, :], T.UG[:, :], "W0 UG", "b6", True, False)
+        for m in range(16):
+            ts(T.E3[:, m, 0:256 - 16 * m], T.KBH[:, 16 * m:256], 2048.0, ALU.add, "KBH BL", "E%d Ed%d" % (m, m), T.BL[:, m:m + 1], ALU.is_equal)
+        ed = " ".join("Ed%d" % m for m in range(16))
+        tt(T.E3[:, :, 0:16], T.E3[:, :, 0:16], T.DM[:, :, :], ALU.mult, ed + " DM", ed)
+        for m in range(15):
+            mm(T.b6[:, 16 * m + 16:256], T.BON[:, :], T.E3[:, m, 16:256 - 16 * m], "BON E%d" % m, "b6", False, False)
+        mm(T.b6[:, 0:256], T.BON[:, :], T.E3[:, :, 0:16], "BON " + ed, "b6", False, True)
+        ts(T.KP[:, :], T.b6[:, 0:256], 0.5, ALU.is_lt, "b6", "KP")
+        scan(T.POS[:, :], T.ZERO[:, :], T.KP[:, :], ALU.max, ALU.add, "ZERO KP", "POS")
+        tt(T.X[:, :], T.KP[:, :], T.POS[:, :], ALU.mult, "KP POS", "X")
+        ts(T.TC[:, 3:4], T.TC[:, 0:1], -1.0, ALU.add, "TC", "TB")
+        ts(T.WJ[:, :], T.JL[:, :], T.TC[:, 0:1], ALU.subtract, "JLx TC", "WJ", 4097.0, ALU.add)
+        tt(T.UJ[:, :], T.JL[:, :], T.BL[:, :], ALU.subtract, "JLx BL", "UJ")
+        for i in range(16):
+            mm(T.b5[:, 0:16], T.LP[:, 128 * i:128 * i + 128], T.X[:, i:256:16], "LP LP%d X" % i, "b5", i == 0, i == 15)
+        if not last:
+            n = T.POS[:, 255:256]
+            ts(T.F4[:, s:32:8], T.ONEF[:, 0:4], n, ALU.mult, "ONEF POS", "F4")
+            cp(T.R8[:, 7 - s:8 - s], n, "POS", "R8")
+            tt(T.TC[:, 0:1], T.TC[:, 0:1], n, ALU.add, "TC POS", "TC")
+            ts(T.TC[:, 1:2], T.TC[:, 0:1], 1.0 / 4096, ALU.mult, "TC", "TC1")
+            prep(t + 1)
+        ts(T.ZT[:, :], T.b5[:, 0:16], 0.0, ALU.is_equal, "b5", "ZT")
+        tt(T.D1[:, :], T.ZT[:, :], T.WJ[:, :], ALU.mult, "ZT WJ", "D1")
+        tt(T.D1[:, :], T.D1[:, :], T.b5[:, 0:16], ALU.add, "D1 b5", "D1")
+        ts(T.DU[:, :], T.D1[:, :], T.TC[:, 3:4], ALU.add, "D1 TB", "DU")
+        do("V", lambda v: v.tensor_copy(T.bankS[:, 0:4352].indirect(T.DU[:, :]), lnd), lk + " DU", "bk bkz")
+
+    def mark(t):
+        ts(T.E1[:, :], T.UJ[:, :], 4112.0, ALU.add, "UJ", "E1")
+        tt(T.E1[:, :], T.E1[:, :], T.ZT[:, :], ALU.mult, "E1 ZT", "E1")
+        tt(T.E1[:, :], T.E1[:, :], T.BL[:, :], ALU.add, "E1 BL", "E1")
+        cp(T.EU[:, :], T.E1[:, :], "E1", "EU")
+        do("V", lambda v: v.tensor_copy(T.USED[:, 0:4368].indirect(T.EU[:, :]), T.ONEI[:, :]), "EU ONEI", "USED USEDx")
+
+    prep(0)
+    ts(T.CL[:, :], T.BON[:, :], col["cval"], ALU.mult, "BON CCv", "CL")
+    lists(0)
+
+    def h0():
+        cp(T.LMF[:, 0:2], T.LM[:, :], "LM", "LMF")
+        ms(T.ONEF[:, :], 1.0, "ONEF")
+        tt(T.LMF[:, 2:3], T.LMF[:, 0:1], T.LMF[:, 1:2], ALU.add, "LMF", "LMF2")
+        tt(T.LMF[:, 3:4], T.LMF[:, 1:2], T.LMF[:, 0:1], ALU.subtract, "LMF", "LMF3")
+        ts(T.NDG[:, :], T.DG[:, :], -1.0, ALU.mult, "DG", "NDG")
+        ts(T.LMF[:, 4:6], T.LMF[:, 2:4], 0.5, ALU.mult, "LMF2 LMF3", "LMF4")
+
+    def h1():
+        ts(T.WCP[:, 0:8], T.IR[:, 0:8], col["grp"], ALU.is_equal, "IR CC", "WCPa")
+        ts(T.WCP[:, 8:16], T.IR[:, 0:8], col["grp"], ALU.is_equal, "IR CC CCw WCPa", "WCP", col["wt"], ALU.mult)
+        for h in (0, 1):
+            ts(T.DM8[:, 256 * h:256 * h + 256], T.GB[0:8, :], CC[0:8, 0:1], ALU.is_equal, "GB CC LMF4", "DM8%d" % h, T.LMF[:, 4 + h:5 + h], ALU.mult)
+
+    def h2():
+        ms(T.RS[:, :], 1.0, "RS")
+        ms(T.RSS[:, :], 1.0, "RSS")
+        ms(T.ZERO[:, :], 0.0, "ZERO")
+        ms(T.RS[:, 0:512:32], 0.0, "RS")
+        ms(T.RSS[:, 0:144:9], 0.0, "RSS")
+        ms(T.K[:, 4096:4112], -32.0, "kinv")
+        cp(T.OC[:, :], T.IR[:, 0:16], "IR", "OC")
+        ts(T.MSK[:, :], T.I9[:, :], col["p8"], ALU.is_equal, "I9 CC", "MSK")
+        ts(T.MI[:, :], T.IF[:, :], col["c16"], ALU.is_equal, "IF CC", "MI")
+        ts(T.RP[:, :], T.IR[:, 0:8], col["p8"], ALU.is_equal, "IR CC", "RP")
+        ts(T.W0C[:, :], T.IR[:, 0:8], col["grp"], ALU.is_equal, "IR CC CCi", "W0C", col["i0"], ALU.mult)
+    build(0, h0, h1)
+    mm(T.b1[:, :], T.ONEF[0:8, :], T.DM8[:, :], "ONEF DM80 DM81", "b1")
+    act(T.MIDT[:, :], T.b1[:, 0:256], AF.Copy, "b1", "MIDT")
+    act(T.HALF[:, :], T.b1[:, 256:512], AF.Copy, "b1", "HALF")
+    pick(0, h2)
+    for i in range(16):
+        act(T.LI[:, 129 * i:128 * i + 128:16], T.WCP[:, 8:16], AF.Copy, "WCP LI", "LI%d" % i)
+    for i in range(16):
+        act(T.LP[:, 129 * i:128 * i + 128:16], T.W0C[:, :], AF.Copy, "W0C LP", "LP%d" % i)
+    ts(T.WBL[:, :], T.IG[:, :], col["grp"], ALU.is_equal, "IG CC CCw", "WBL", col["wt"], ALU.mult)
+    ts(T.W0[:, :], T.BON[:, :], col["i0"], ALU.mult, "BON CCi", "W0")
+    ts(T.DM[:, :, :], T.I16[:, :, :], col["i"], ALU.is_gt, "I16 CC", "DM")
+    ts(T.JL[:, :], T.JL[:, :], col["i"], ALU.add, "JL CC", "JLx")
+    masks(1)
+    keep(0)
+    for t in range(1, RO):
+        lists(t)
+        build(t, lambda: None, lambda: None)
+        pick(t, lambda: None)
+        mark(t - 1)
+        if t + 1 < RO:
+            masks(t + 1)
+        keep(t)
+    dma("S", "out", T.y[:, :], T.bankS[:, B:4096], "bk bkz", "out")
+    for t in range(RO):
+        g.wait_ge(T.sem["sent%d" % t], 14)
+    for e in ("V", "A", "P", "G"):
+        g.wait_ge(T.sem["s" + e], cnt[e])
+    for n in _DMAS:
+        g.wait_ge(T.sem["d_" + n], 16)

@@ -4,20 +4,22 @@ from concourse.mybir import dt, AluOpType as ALU, AxisListType as AX, Activation
 B, J, CAP, RO, NR = 3072, 4096, 32, 4, 8
 M1 = 1.5 * 2.0 ** 23
 MN = 1.5 * 2.0 ** 16
+M256 = 1.5 * 2.0 ** 15
 M32 = 1.5 * 2.0 ** 28
 M4096 = 1.5 * 2.0 ** 35
 MID = 1920
+NA = 12
 SEG = 41
 f32, bf, i32, u16, f16 = "float32", "bfloat16", "int32", "uint16", "float16"
 
 SCRATCH = {}
 for _d, _l in (
-    (bf, "bankS 4352,K 4112,YG 4096,FX 4096,XG 4096,ONE 256,ZERO 256,TRI 128,BID 128,DG 128,NDG 128,WCP 16,W0C 8,WBL 128,BON 128,W0 128,LI 2048,LP 2048,"
-         "COLT 256,CL 128,DM 16 16,RS 512,RSS 144,MSK 144,MI 256,JC 1,RH 256,LQ 1024,OWN 256,O 2048,S4 256,U 2048,Z 328,EO 512,CU 512,IN 512,C2 512,SMM 144,SS 144,UG 256,"
-         "E3 16 272,KP 256,POS 256,X 256,send 1024,land 1024"),
+    (bf, "bankS 4352,K 4112,YG 4096,FX 4096,XG 4096,ZG 512,ONE 256,ZERO 256,TRI 128,BID 128,DG 128,NDG 128,WCP 16,W0C 8,WBL 128,BON 128,W0 128,LI 2048,LP 2048,"
+         "COLT 256,CL 128,DM 16 16,RS 512,RSS 144,MSK 144,MI 256,JC 1,RH 256,IND 128,LQ 1024,OWN 256,O 2048,S4 256,U 2048,Z 328,EO 512,CU 512,IN 512,C2 512,SMM 144,SS 144,UG 256,"
+         "E3 16 272,POS 256,X 256,send 1024,land 1024"),
     (i32, "USED 4368,RA 1024,RB 1024,RC 1024,PID 1,TI 8,ONEI 256,OI 256,OJ 256,KLI 16,KLJ 16"),
     (f32, "CC 32,IR 256,IG 128,II 128,GB 256,I16 16 16,IF 256,I9 144,JL 16,ONEF 128,MK 8,MD 8,MS 8,MQ 128,RQ 32,NEGM 8,IT 128,MIDT 256,HALF 256,F4 32,R8 8,TC 8,PP 8,PR 8,"
-          "SEL 16,SM 8,CS 16,DQ 32,DS 32,HI 4,LO 4,CIT 128,W1 256,V1 256,Z1 256,J16 16,R32 16,INV 16,BL 16,ZT 16,WJ 16,D1 16,UJ 16,E1 16"),
+          "SEL 16,SM 8,CS 16,DQ 32,DS 32,HI 4,LO 4,RCF 1024,OA 256,W1 256,V1 256,Z1 256,J16 16,R32 16,INV 16,BL 16,ZT 16,WJ 16,D1 16,UJ 16,E1 16"),
     (u16, "OX 256,OY 256,OZ 256,OFJ 16,BU 16,DU 16,EU 16,OC 16"),
     (f16, "RP 8,LJ 256,KBH 256"),
 ):
@@ -145,16 +147,17 @@ def rank_program(g, core, T, topo):
     CC = T.CC
     col = {n: CC[:, k:k + 1] for k, n in enumerate(
         ["pid", "i", "m", "typ", "grp", "p8", "c16", "wt", "podd", "sgs", "msg", "off", "tm1", "cval", "i0",
-         "mm1", "sm0", "sm1", "sm2", "sm3", "t0", "t1", "c32"])}
+         "mm1", "sm0", "sm1", "sm2", "sm3", "t0", "t1", "c32", "m15", "on1"])}
     for k, (sh, an) in enumerate([(0, 255), (0, 15), (1, 7), (0, 1), (4, 7), (0, 7), (3, 15)]):
         ts(T.TI[:, k:k + 1], T.PID[:, :], sh, ALU.arith_shift_right, "PID", "TI%d" % k, an, ALU.bitwise_and)
     cp(CC[:, 0:7], T.TI[:, 0:7], "TI0 TI1 TI2 TI3 TI4 TI5 TI6", "CC")
-    for n, src, a, b, key in (("tm1", "typ", 1.0, -1.0, "CCt"), ("sm0", "m", -1.0, 3.0, "CCx0"), ("mm1", "m", 1.0, -1.0, "CCn"), ("msg", "typ", -2.0, 1.0, "CCm"),
+    for n, src, a, b, key in (("tm1", "typ", 1.0 / 256, -1.0 / 256, "CCt"), ("sm0", "m", -1.0, 3.0, "CCx0"), ("mm1", "m", 1.0, -1.0, "CCn"), ("msg", "typ", -2.0, 1.0, "CCm"),
                               ("off", "typ", -1.0, 1.0, "CCf"), ("wt", "i", 14.0, 9.0, "CCw"), ("sm1", "m", -1.0, 4.0, "CCx1"), ("sm2", "m", -1.0, 5.0, "CCx2"),
-                              ("sm3", "m", -1.0, 6.0, "CCx3"), ("podd", "p8", 2.0, 1.0, "CCo"), ("c32", "c16", 1.0, 16.0, "CC2")):
+                              ("sm3", "m", -1.0, 6.0, "CCx3"), ("podd", "p8", 2.0, 1.0, "CCo"), ("c32", "c16", 1.0, 16.0, "CC2"),
+                              ("m15", "pid", 0.0, -15.0, "CCg"), ("on1", "pid", 0.0, 1.0, "CCh")):
         act(col[n], col[src], AF.Copy, "CC", key, a, b)
         if n == "mm1":
-            act(T.COLT[:, :], T.IR[:, :], AF.Identity, "IR CCt", "COLT", 1.0, col["tm1"])
+            act(T.COLT[:, :], T.IR[:, :], AF.Identity, "IR CCt", "COLT", 1.0 / 256, col["tm1"])
     act(T.JC[:, :], col["pid"], AF.Copy, "CC", "JC")
     ts(col["sgs"], col["typ"], 2.0 / 4096, ALU.mult, "CC", "CCs", -1.0 / 4096, ALU.add)
     ts(T.BON[:, :], T.IG[:, :], col["grp"], ALU.is_equal, "IG CC", "BON")
@@ -199,99 +202,114 @@ def rank_program(g, core, T, topo):
     tt(col["cval"], col["cval"], col["t1"], ALU.add, "CCv CC1", "CCv")
 
     bankk = "bk bkz"
+    win = T.bankS[:, 0:4096]
     c0 = -(MID + 0.5) + 2.0 ** -13
     F4k, R8k = "F4 F40 F41 F42 F43", "R8 R80 R81 R82 R83"
 
-    def prep(t):
+    def prep(t, app=()):
+        app = list(app) + [lambda: None] * (5 - len(app))
         s = 4 + t
         CS, SEL = T.CS, T.SEL
         ct = SEL[:, s:s + 1]
         c = slice(256 * t, 256 * t + 256)
-        tt(T.PP[:, 0:s], T.F4[:, 0:s], T.R8[:, 8 - s:8], ALU.mult, F4k + " " + R8k, "PP")
         tt(T.DQ[:, :], T.F4[:, :], T.MQ[:, 32 * t:32 * t + 32], ALU.mult, F4k + " MQ%d MQ%da MQ%db MQ%dc" % (t, t, t, t), "DQ")
-        ts(T.PR[:, 0:s], T.PP[:, 0:s], -2047.5, ALU.add, "PP", "PR", M4096, ALU.add)
+        tt(T.PP[:, 0:s], T.F4[:, 0:s], T.R8[:, 8 - s:8], ALU.mult, F4k + " " + R8k, "PP")
         scan(T.DS[:, :], T.RQ[:, :], T.DQ[:, :], ALU.mult, ALU.add, "RQ DQ", "DS")
+        ts(T.PR[:, 0:s], T.PP[:, 0:s], -2047.5, ALU.add, "PP", "PR", M4096, ALU.add)
         scan(SEL[:, 1:s + 1], T.PR[:, 0:s], T.NEGM[:, 0:s], ALU.add, ALU.add, "PR NEGM", "SEL")
         ts(T.HI[:, 0:2], T.DS[:, 7:16:8], MN, ALU.add, "DS", "HI", MN, ALU.subtract)
-        ts(CS[:, 0:1], ct, 1.0 / 256, ALU.mult, "SEL", "CS0")
         tt(T.SM[:, :], SEL[:, 0:8], T.MK[:, :], ALU.mult, "SEL MK", "SM")
-        do("V", lambda v: v.reciprocal(CS[:, 1:2], CS[:, 0:1]), "CS0", "CS1")
+        do("V", lambda v: v.reciprocal(CS[:, 1:2], ct), "SEL", "CS1")
         do("V", lambda v: v.tensor_reduce(CS[:, 2:3], T.SM[:, :], AX.X, ALU.add), "SM", "CS2")
         ts(T.HI[:, 2:4], T.DS[:, 23:32:8], M32, ALU.add, "DS", "HI2", M32, ALU.subtract)
-        ts(CS[:, 3:4], CS[:, 2:3], CS[:, 1:2], ALU.mult, "CS1 CS2", "CS3", -0.46875, ALU.add)
+        app[0]()
+        ts(CS[:, 3:4], CS[:, 2:3], CS[:, 1:2], ALU.mult, "CS1 CS2", "CS3", -0.46875 / 256, ALU.add)
+        app[1]()
         tt(T.LO[:, :], T.DS[:, 7:32:8], T.HI[:, :], ALU.subtract, "DS HI HI2", "LO")
-        ts(CS[:, 4:5], CS[:, 3:4], M1, ALU.add, "CS3", "CS4", M1, ALU.subtract)
-        ts(T.Z1[:, :], T.RC[:, c], T.TC[:, 1:2], ALU.mult, "RC%d TC1" % (t > 0), "Z1", c0, ALU.add)
-        ts(CS[:, 5:6], CS[:, 4:5], CS[:, 0:1], ALU.mult, "CS0 CS2 CS4", "CS5", CS[:, 2:3], ALU.subtract)
+        ts(CS[:, 4:5], CS[:, 3:4], M256, ALU.add, "CS3", "CS4", M256, ALU.subtract)
+        if t:
+            act(T.Z1[:, :], T.RCF[:, c], AF.Copy, "RCF TC1", "Z1", T.TC[:, 1:2], c0)
+        else:
+            ts(T.Z1[:, :], T.RC[:, c], T.TC[:, 1:2], ALU.mult, "RC0 TC1", "Z1", c0, ALU.add)
+        app[2]()
+        ts(CS[:, 5:6], CS[:, 4:5], ct, ALU.mult, "SEL CS2 CS4", "CS5", CS[:, 2:3], ALU.subtract)
+        app[3]()
         ts(T.OZ[:, :], T.Z1[:, :], M1, ALU.add, "Z1", "OZ", M1 - MID, ALU.subtract)
         ts(CS[:, 6:7], CS[:, 5:6], col["msg"], ALU.mult, "CS5 CCm CCf", "CS6", col["off"], ALU.add)
+        app[4]()
 
     def lists(t):
         CS, ct, k = T.CS, T.SEL[:, 4 + t:5 + t], "%d" % (t > 0)
         c = slice(256 * t, 256 * t + 256)
-        ts(T.CIT[:, :], T.IT[:, :], ct, ALU.mult, "IT SEL", "CIT")
         ts(T.RH[:, :], T.COLT[:, :], CS[:, 4:5], ALU.is_ge, "COLT CS4", "RH")
+        ts(T.IND[:, :], T.IT[:, :], ct, ALU.mult, "IT SEL CS6", "IND", CS[:, 6:7], ALU.is_ge)
         for b in ("b2", "b4"):
             mm(T[b][:, 0:256], T.CL[:, :], T.ONE[:, :], "CL ONE", b, True, False)
         for q, b in ((1, "b1"), (3, "b2"), (0, "b3"), (2, "b4")):
-            for h, src in ((0, "HI"), (1, "LO")):
+            for h in (0, 1):
                 n = 2 * q + h
-                ts(T.LQ[:, 128 * n:128 * n + 128], T.CIT[:, :], CS[:, 6:7], ALU.is_ge, "CIT CS6 HI HI2 LO", "LQ%d" % n, T[src][:, q:q + 1], ALU.mult)
+                if h == 0:
+                    ts(T.LQ[:, 128 * n:128 * n + 128], T.IND[:, :], T.HI[:, q:q + 1], ALU.mult, "IND HI HI2", "LQ%d" % n)
+                else:
+                    act(T.LQ[:, 128 * n:128 * n + 128], T.IND[:, :], AF.Copy, "IND LO", "LQ%d" % n, T.LO[:, q:q + 1])
                 mm(T[b][:, 0:256], T.LQ[:, 128 * n:128 * n + 128], T.RH[:, :], "LQ%d RH" % n, b, q < 2 and h == 0, h == 1)
+        act(T.ZG[:, :], win.indirect(T.OZ[:, 192:224]), AF.Copy, "OZ " + bankk, "ZG")
         for w, r, o, bn, bs in (("V1", "RB", "OY", "b1", "b2"), ("W1", "RA", "OX", "b3", "b4")):
             tt(T[w][:, :], T[bn][:, 0:256], T[r][:, c], ALU.mult, bn + " " + r + k, w)
             tt(T[w][:, :], T[w][:, :], T[bs][:, 0:256], ALU.add, w + " " + bs, w)
             ts(T[o][:, :], T[w][:, :], M1, ALU.add, w, o, M1 - MID, ALU.subtract)
-
-    win = T.bankS[:, 0:4096]
 
     def build(t, h0, h1):
         def y(q, dst="YG", lst="OY", a=0, n=1024):
             o = 1024 * q + a
             act(T[dst][:, o:o + n], win.indirect(T[lst][:, o // 16:(o + n) // 16]), AF.Copy, lst + " " + bankk, "%s%d%d" % (dst, q, a))
 
-        def x(q, a=0):
-            o = slice(1024 * q + a, 1024 * q + 1024)
-            tt(T.FX[:, o], win.indirect(T.OX[:, 64 * q + a // 16:64 * q + 64]), T.YG[:, o], (ALU.min, ALU.max, None, ALU.add)[q], "OX YG%d%d " % (q, a) + bankk, "FX%d%d" % (q, a))
+        def x(q, a=0, n=1024):
+            o = slice(1024 * q + a, 1024 * q + a + n)
+            tt(T.FX[:, o], win.indirect(T.OX[:, 64 * q + a // 16:64 * q + (a + n) // 16]), T.YG[:, o], (ALU.min, ALU.max, None, ALU.add)[q], "OX YG%d%d " % (q, a) + bankk, "FX%d%d" % (q, a))
 
         def both(q, b, o, lh):
-            mm(T[b][:, :], T.DG[:, :], T.XG[:, o:o + 512], "DG XG%d0" % q, b, True, False)
-            mm(T[b][:, :], T[lh][:, :], T.YG[:, o:o + 512], "%s YG%d0" % (lh, q), b, False, True)
+            k = (q, o - 1024 * q)
+            mm(T[b][:, :], T.DG[:, :], T.XG[:, o:o + 512], "DG XG%d%d" % k, b, True, False)
+            mm(T[b][:, :], T[lh][:, :], T.YG[:, o:o + 512], lh + " YG%d%d" % k, b, False, True)
 
         def z(q, a=0, n=1024):
             o = 1024 * q + a
             tt(T.K[:, o:o + n], win.indirect(T.OZ[:, o // 16:(o + n) // 16]), T.FX[:, o:o + n], ALU.min, "OZ FX%d%d FX%d512 " % (q, a, q) + bankk, "K%d%d" % (q, a))
 
-        def sums(q):
+        def sums(q, n=1024):
             for b in range(32):
-                mm(T.b0[32 * q:32 * q + 32, b:512:32], T.K[:, 1024 * q + b:1024 * q + 1024:32], T.WCP[:, :], "WCP K%d0 K%d512" % (q, q), "b0")
-        y(0)
+                mm(T.b0[32 * q:32 * q + n // 32, b:512:32], T.K[:, 1024 * q + b:1024 * q + n:32], T.WCP[:, :], "WCP K%d0 K%d512" % (q, q), "b0")
+        y(0, n=512)
+        y(0, a=512, n=512)
         y(1)
+        x(0, 0, 512)
+        x(0, 512, 512)
         h0()
-        x(0)
         h1()
-        y(2)
-        y(2, "XG", "OX")
         z(0)
-        both(2, "b5", 2048, "NDG")
-        both(2, "b6", 2560, "NDG")
         sums(0)
+        for a, b in ((0, "b5"), (512, "b6")):
+            y(2, a=a, n=512)
+            y(2, "XG", "OX", a=a, n=512)
+            both(2, b, 2048 + a, "NDG")
         x(1)
+        z(1)
         y(3, a=512, n=512)
+        act(T.FX[:, 2048:2560], T.b5[:, :], AF.Abs, "b5", "FX20")
+        act(T.FX[:, 2560:3072], T.b6[:, :], AF.Abs, "b6", "FX2512")
+        sums(1)
+        x(3, 512, 512)
+        z(3, 512, 512)
+        if t:
+            sums(3)
         y(3, n=512)
         y(3, "XG", "OX", n=512)
         both(3, "b7", 3072, "DG")
-        act(T.FX[:, 2048:2560], T.b5[:, :], AF.Abs, "b5", "FX20")
-        act(T.FX[:, 2560:3072], T.b6[:, :], AF.Abs, "b6", "FX2512")
-        act(T.FX[:, 3072:3584], T.b7[:, :], AF.Copy, "b7", "FX30")
-        z(1)
-        sums(1)
-        x(3, 512)
-        z(3, 512, 512)
         z(2)
         sums(2)
-        z(3, 0, 512)
-        sums(3)
+        tt(T.K[:, 3072:3584], T.b7[:, :], T.ZG[:, :], ALU.min, "b7 ZG", "K30")
+        sums(3, 512 if t else 1024)
 
     def pick(t, h):
         tt(T.Z1[:, :], T.b0[:, 0:256], T.MIDT[:, :], ALU.subtract, "b0 MIDT", "Z1")
@@ -300,7 +318,9 @@ def rank_program(g, core, T, topo):
         ts(T.OJ[:, :], T.OI[:, :], 15, ALU.bitwise_and, "OI", "OJ")
         tt(T.b7[:, 256:512], T.b7[:, 0:256], T.HALF[:, :], ALU.is_le, "b7 HALF", "b7")
         tt(T.OWN[:, :], T.OJ[:, :], T.b7[:, 256:512], ALU.mult, "OJ b7", "OWN")
-        for p in range(8):
+        act(T.OA[:, :], T.OWN[:, :], AF.Abs, "OWN CCg", "OA", 1.0, col["m15"])
+        act(T.O[:, 1792:2048], T.OA[:, :], AF.Relu, "OA CCh", "O7", -1.0, col["on1"])
+        for p in range(7):
             ts(T.O[:, 256 * p:256 * p + 256], T.OWN[:, :], 2.0 * p + 1, ALU.is_equal, "OWN", "O%d" % p)
         h()
         for q in range(8):
@@ -316,16 +336,17 @@ def rank_program(g, core, T, topo):
         for c in range(8):
             ts(T.U[:, 256 * c:256 * c + 256], T.S4[:, :], 4.0 * c, ALU.is_le, "S40 S41 S42 S43", "U%d" % c)
         for ch in (0, 1):
-            for lo, hi, b in ((9, SEG, "b%d" % (1 + ch)), (0, 9, "b%d" % (3 + ch))):
+            for lo, hi, b in ((0, 9, "b%d" % (3 + ch)), (9, SEG, "b%d" % (1 + ch))):
                 for q in range(8):
                     mm(T[b][:, (hi - lo) * q:(hi - lo) * (q + 1)], T.U[:, 1024 * ch + q:1024 * ch + 1024:8], T.Z[:, SEG * q + lo:SEG * q + hi],
                        "Z U%d U%d U%d U%d" % tuple(range(4 * ch, 4 * ch + 4)), b)
         for ch in (0, 1):
             d, b = slice(72 * ch, 72 * ch + 72), T["b%d" % (3 + ch)]
-            ts(T.EO[:, 256 * ch:256 * ch + 256], T["b%d" % (1 + ch)][:, 0:256], col["podd"], ALU.is_equal, "b%d CCo" % (1 + ch), "EO%d" % ch)
             tt(T.SMM[:, d], b[:, 0:72], T.MSK[:, d], ALU.mult, "b%d MSK" % (3 + ch), "SMM%d" % ch)
-            ts(T.R32[:, 8 * ch:8 * ch + 8], b[:, 8:72:9], 32.0, ALU.mult, "b%d" % (3 + ch), "R32%d" % ch, -2048.0, ALU.add)
-        scan(T.SS[:, :], T.RSS[:, :], T.SMM[:, :], ALU.mult, ALU.add, "RSS SMM0 SMM1", "SS")
+            act(T.R32[:, 8 * ch:8 * ch + 8], b[:, 8:72:9], AF.Copy, "b%d" % (3 + ch), "R32%d" % ch, 32.0, -2048.0)
+            if ch:
+                scan(T.SS[:, :], T.RSS[:, :], T.SMM[:, :], ALU.mult, ALU.add, "RSS SMM0 SMM1", "SS")
+            ts(T.EO[:, 256 * ch:256 * ch + 256], T["b%d" % (1 + ch)][:, 0:256], col["podd"], ALU.is_equal, "b%d CCo" % (1 + ch), "EO%d" % ch)
         tt(T.EO[:, 0:512:32], T.EO[:, 0:512:32], T.SS[:, 8:144:9], ALU.add, "SS EO0 EO1", "EO0 EO1")
         scan(T.CU[:, :], T.RS[:, :], T.EO[:, :], ALU.mult, ALU.add, "RS EO0 EO1", "CU")
         ts(T.IN[:, 0:256], T.CU[:, 0:256], col["c16"], ALU.is_le, "CU CC", "IN0")
@@ -356,49 +377,63 @@ def rank_program(g, core, T, topo):
         s, last = 4 + t, t == RO - 1
         o, lk = 256 * t, "lnd%d" % t
         lnd = T.land[:, o:o + 256]
+        ts(T.TC[:, 3:4], T.TC[:, 0:1], -1.0, ALU.add, "TC", "TB")
+        ts(T.WJ[:, :], T.JL[:, :], T.TC[:, 0:1], ALU.subtract, "JLx TC", "WJ", 4097.0, ALU.add)
         wait("P", "arr%d" % t, 14)
         mm(T.b3[:, 0:256], T.WBL[:, :], lnd, "WBL " + lk, "b3")
         for i in range(16):
             mm(T.b4[:, 0:16], T.LI[:, 128 * i:128 * i + 128], T.land[:, o + i:o + 256:16], "LI LI%d " % i + lk, "b4", i == 0, i == 15)
         cp(T.OI[:, :], T.b3[:, 0:256], "b3", "OI")
         ts(T.OJ[:, :], T.OI[:, :], 3, ALU.arith_shift_right, "OI", "OJ", 4095, ALU.bitwise_and)
-        ts(T.KBH[:, :], T.OJ[:, :], -2048.0, ALU.add, "OJ", "KBH")
         cp(T.KLI[:, :], T.b4[:, 0:16], "b4", "KLI")
-        ts(T.INV[:, :], T.b4[:, 0:16], 0.0, ALU.is_lt, "b4", "INV", 4096.0, ALU.mult)
+        ts(T.KBH[:, :], T.OJ[:, :], -2048.0, ALU.add, "OJ", "KBH")
         ts(T.KLJ[:, :], T.KLI[:, :], 3, ALU.arith_shift_right, "KLI", "KLJ", 4095, ALU.bitwise_and)
+        ts(T.INV[:, :], T.b4[:, 0:16], 0.0, ALU.is_lt, "b4", "INV", 4096.0, ALU.mult)
         tt(T.BL[:, :], T.KLJ[:, :], T.INV[:, :], ALU.max, "KLJ INV", "BL")
-        cp(T.BU[:, :], T.BL[:, :], "BL", "BU")
-        do("V", lambda v: v.tensor_copy(T.UG[:, :], T.USED[:, 0:4112].indirect(T.BU[:, :])), "USED USEDx BU", "UG")
-        mm(T.b6[:, 0:256], T.W0[:, :], T.UG[:, :], "W0 UG", "b6", True, False)
+
+        def ed(a, b):
+            return " ".join("Ed%d" % m for m in range(a, b))
+
+        def later(a, b):
+            tt(T.E3[:, a:b, 0:16], T.E3[:, a:b, 0:16], T.DM[:, a:b, :], ALU.mult, ed(a, b) + " DM", ed(a, b))
         for m in range(16):
             ts(T.E3[:, m, 0:256 - 16 * m], T.KBH[:, 16 * m:256], 2048.0, ALU.add, "KBH BL", "E%d Ed%d" % (m, m), T.BL[:, m:m + 1], ALU.is_equal)
-        ed = " ".join("Ed%d" % m for m in range(16))
-        tt(T.E3[:, :, 0:16], T.E3[:, :, 0:16], T.DM[:, :, :], ALU.mult, ed + " DM", ed)
+            if m == 0:
+                cp(T.BU[:, :], T.BL[:, :], "BL", "BU")
+            if m == 1:
+                do("V", lambda v: v.tensor_copy(T.UG[:, :], T.USED[:, 0:4112].indirect(T.BU[:, :])), "USED USEDx BU", "UG")
+                mm(T.b6[:, 0:256], T.W0[:, :], T.UG[:, :], "W0 UG", "b6", True, False)
+            if m == NA + 1:
+                later(0, NA)
+        later(NA, 16)
         for m in range(15):
             mm(T.b6[:, 16 * m + 16:256], T.BON[:, :], T.E3[:, m, 16:256 - 16 * m], "BON E%d" % m, "b6", False, False)
-        mm(T.b6[:, 0:256], T.BON[:, :], T.E3[:, :, 0:16], "BON " + ed, "b6", False, True)
-        ts(T.KP[:, :], T.b6[:, 0:256], 0.5, ALU.is_lt, "b6", "KP")
-        scan(T.POS[:, :], T.ZERO[:, :], T.KP[:, :], ALU.max, ALU.add, "ZERO KP", "POS")
-        tt(T.X[:, :], T.KP[:, :], T.POS[:, :], ALU.mult, "KP POS", "X")
-        ts(T.TC[:, 3:4], T.TC[:, 0:1], -1.0, ALU.add, "TC", "TB")
-        ts(T.WJ[:, :], T.JL[:, :], T.TC[:, 0:1], ALU.subtract, "JLx TC", "WJ", 4097.0, ALU.add)
-        tt(T.UJ[:, :], T.JL[:, :], T.BL[:, :], ALU.subtract, "JLx BL", "UJ")
-        for i in range(16):
-            mm(T.b5[:, 0:16], T.LP[:, 128 * i:128 * i + 128], T.X[:, i:256:16], "LP LP%d X" % i, "b5", i == 0, i == 15)
+        mm(T.b6[:, 0:256], T.BON[:, :], T.E3[:, :, 0:16], "BON " + ed(0, 16), "b6", False, True)
+        ts(T.b7[:, 0:256], T.b6[:, 0:256], 0.5, ALU.is_lt, "b6", "b7")
+        scan(T.POS[:, :], T.ZERO[:, :], T.b7[:, 0:256], ALU.max, ALU.add, "ZERO b7", "POS")
+        n = T.POS[:, 255:256]
         if not last:
-            n = T.POS[:, 255:256]
+            tt(T.TC[:, 0:1], T.TC[:, 0:1], n, ALU.add, "TC POS", "TC")
             ts(T.F4[:, s:32:8], T.ONEF[:, 0:4], n, ALU.mult, "ONEF POS", "F4")
             cp(T.R8[:, 7 - s:8 - s], n, "POS", "R8")
-            tt(T.TC[:, 0:1], T.TC[:, 0:1], n, ALU.add, "TC POS", "TC")
+        tt(T.X[:, :], T.b7[:, 0:256], T.POS[:, :], ALU.mult, "b7 POS", "X")
+        if not last:
             ts(T.TC[:, 1:2], T.TC[:, 0:1], 1.0 / 4096, ALU.mult, "TC", "TC1")
-            prep(t + 1)
-        ts(T.ZT[:, :], T.b5[:, 0:16], 0.0, ALU.is_equal, "b5", "ZT")
-        tt(T.D1[:, :], T.ZT[:, :], T.WJ[:, :], ALU.mult, "ZT WJ", "D1")
-        tt(T.D1[:, :], T.D1[:, :], T.b5[:, 0:16], ALU.add, "D1 b5", "D1")
-        ts(T.DU[:, :], T.D1[:, :], T.TC[:, 3:4], ALU.add, "D1 TB", "DU")
-        do("V", lambda v: v.tensor_copy(T.bankS[:, 0:4352].indirect(T.DU[:, :]), lnd), lk + " DU", "bk bkz")
+        for i in range(16):
+            mm(T.b5[:, 0:16], T.LP[:, 128 * i:128 * i + 128], T.X[:, i:256:16], "LP LP%d X" % i, "b5", i == 0, i == 15)
+        app = (lambda: ts(T.ZT[:, :], T.b5[:, 0:16], 0.0, ALU.is_equal, "b5", "ZT"),
+               lambda: tt(T.D1[:, :], T.ZT[:, :], T.WJ[:, :], ALU.mult, "ZT WJ", "D1"),
+               lambda: tt(T.D1[:, :], T.D1[:, :], T.b5[:, 0:16], ALU.add, "D1 b5", "D1"),
+               lambda: ts(T.DU[:, :], T.D1[:, :], T.TC[:, 3:4], ALU.add, "D1 TB", "DU"),
+               lambda: do("V", lambda v: v.tensor_copy(T.bankS[:, 0:4352].indirect(T.DU[:, :]), lnd), lk + " DU", "bk bkz"))
+        if last:
+            for f in app:
+                f()
+        else:
+            prep(t + 1, app)
 
     def mark(t):
+        tt(T.UJ[:, :], T.JL[:, :], T.BL[:, :], ALU.subtract, "JLx BL", "UJ")
         ts(T.E1[:, :], T.UJ[:, :], 4112.0, ALU.add, "UJ", "E1")
         tt(T.E1[:, :], T.E1[:, :], T.ZT[:, :], ALU.mult, "E1 ZT", "E1")
         tt(T.E1[:, :], T.E1[:, :], T.BL[:, :], ALU.add, "E1 BL", "E1")
@@ -449,14 +484,13 @@ def rank_program(g, core, T, topo):
     ts(T.DM[:, :, :], T.I16[:, :, :], col["i"], ALU.is_gt, "I16 CC", "DM")
     ts(T.JL[:, :], T.JL[:, :], col["i"], ALU.add, "JL CC", "JLx")
     masks(1)
+    cp(T.RCF[:, 256:1024], T.RC[:, 256:1024], "RC1", "RCF")
     keep(0)
     for t in range(1, RO):
         lists(t)
         build(t, lambda: None, lambda: None)
-        pick(t, lambda: None)
+        pick(t, lambda: masks(t + 1) if t + 1 < RO else None)
         mark(t - 1)
-        if t + 1 < RO:
-            masks(t + 1)
         keep(t)
     dma("S", "out", T.y[:, :], T.bankS[:, B:4096], "bk bkz", "out")
     for t in range(RO):

from concourse.bass import DstId, RemoteDMATransfer
from concourse.mybir import dt, AluOpType as ALU, AxisListType as AX, ActivationFunctionType as AF

B, J, CAP, RO, NR = 3072, 4096, 32, 4, 8
M1 = 1.5 * 2.0 ** 23
MN = 1.5 * 2.0 ** 16
M256 = 1.5 * 2.0 ** 15
M32 = 1.5 * 2.0 ** 28
M4096 = 1.5 * 2.0 ** 35
MID = 1920
NA = 12
SEG = 41
f32, bf, i32, u16, f16 = "float32", "bfloat16", "int32", "uint16", "float16"

SCRATCH = {}
for _d, _l in (
    (bf, "bankS 4352,K 4112,YG 4096,FX 4096,XG 4096,ZG 512,ONE 256,ZERO 256,TRI 128,BID 128,DG 128,NDG 128,WCP 16,W0C 8,WBL 128,BON 128,W0 128,LI 2048,LP 2048,"
         "COLT 256,CL 128,DM 16 16,RS 512,RSS 144,MSK 144,MI 256,JC 1,RH 256,IND 128,LQ 1024,OWN 256,O 2048,S4 256,U 2048,Z 328,EO 512,CU 512,IN 512,C2 512,SMM 144,SS 144,UG 256,"
         "E3 16 272,POS 256,X 256,send 1024,land 1024"),
    (i32, "USED 4368,RA 1024,RB 1024,RC 1024,PID 1,TI 8,ONEI 256,OI 256,OJ 256,KLI 16,KLJ 16"),
    (f32, "CC 32,IR 256,IG 128,II 128,GB 256,I16 16 16,IF 256,I9 144,JL 16,ONEF 128,MK 8,MD 8,MS 8,MQ 128,RQ 32,NEGM 8,IT 128,MIDT 256,HALF 256,F4 32,R8 8,TC 8,PP 8,PR 8,"
          "SEL 16,SM 8,CS 16,DQ 32,DS 32,HI 4,LO 4,RCF 1024,OA 256,W1 256,V1 256,Z1 256,J16 16,R32 16,INV 16,BL 16,ZT 16,WJ 16,D1 16,UJ 16,E1 16"),
    (u16, "OX 256,OY 256,OZ 256,OFJ 16,BU 16,DU 16,EU 16,OC 16"),
    (f16, "RP 8,LJ 256,KBH 256"),
):
    for _x in _l.split(","):
        _x = _x.split()
        SCRATCH[_x[0]] = ("sbuf", [128] + [int(v) for v in _x[1:]], _d)
SCRATCH.update({"NL": ("sbuf", [8, 4], i32), "LM": ("sbuf", [8, 2], i32), "NLF": ("sbuf", [8, 4], f32), "LMF": ("sbuf", [8, 8], f32),
                "SL8": ("sbuf", [8, 128], f32), "DM8": ("sbuf", [8, 512], f32)})
for _k in range(8):
    SCRATCH["b%d" % _k] = ("psum", [128, 512], f32)
_DMAS = ["ncl", "lim", "bank", "ra0", "rb0", "rc0", "ra1", "rb1", "rc1", "used", "out"]
SEMAPHORES = ["sV", "sA", "sP", "sG"] + ["d_" + n for n in _DMAS] + ["arr%d" % t for t in range(RO)] + ["sent%d" % t for t in range(RO)]
BANKS = tuple("b%d" % k for k in range(8))


def rank_program(g, core, T, topo):
    rank = T.rank_of(core)
    if rank is None:
        return
    eng = {"V": g.vector, "A": g.scalar, "P": g.tensor, "G": g, "S": g.sync}
    cnt = {"V": 0, "A": 0, "P": 0, "G": 0}
    seen = {e: {} for e in eng}
    lastw, readers = {}, {}

    def wait(e, sem, val):
        if seen[e].get(sem, 0) < val:
            eng[e].wait_ge(T.sem[sem], val)
            seen[e][sem] = val

    def order(e, r, w):
        req = {}
        me = "s" + e

        def add(ev):
            if ev is not None:
                req[ev[0]] = max(req.get(ev[0], 0), ev[1])
        for k in r:
            add(lastw.get(k))
        for k in list(w) + [k for k in r if k in BANKS]:
            add(lastw.get(k))
            for ev in readers.get(k, {}).items():
                if ev[0] != me:
                    add(ev)
        if e == "P":
            req.pop("sP", None)
        for sem in sorted(req):
            wait(e, sem, req[sem])

    def note(ev, r, w):
        for k in r:
            readers.setdefault(k, {})[ev[0]] = ev[1]
        for k in w:
            lastw[k] = ev
            readers[k] = {}

    def do(e, call, r, w):
        r, w = r.split(), w.split()
        order(e, r, w)
        cnt[e] += 1
        call(eng[e]).then_inc(T.sem["s" + e], 1)
        note(("s" + e, cnt[e]), r, w)

    def dma(e, name, out, in_, r, w):
        r, w = r.split(), w.split()
        order(e, r, w)
        eng[e].dma_start(out, in_).then_inc(T.sem["d_" + name], 16)
        note(("d_" + name, 16), r, w)

    def ts(out, in0, s1, op0, r, w, s2=None, op1=None):
        if op1 is None:
            do("V", lambda v: v.tensor_scalar(out, in0, s1, None, op0), r, w)
        else:
            do("V", lambda v: v.tensor_scalar(out, in0, s1, s2, op0, op1), r, w)

    def tt(out, a, b, op, r, w):
        do("V", lambda v: v.tensor_tensor(out, a, b, op), r, w)

    def cp(out, a, r, w):
        do("V", lambda v: v.tensor_copy(out, a), r, w)

    def ms(ap, c, w):
        do("V", lambda v: v.memset(ap, c), "", w)

    def mm(out, l, rh, r, w, start=True, stop=True):
        do("P", lambda p: p.matmul(out, l, rh, start, stop), r, w)

    def act(out, a, fn, r, w, scale=1.0, bias=0.0):
        do("A", lambda s: s.activation(out, a, fn, bias=bias, scale=scale), r, w)

    def iota(ap, pat, cm, w, base=0):
        do("G", lambda q: q.iota(ap, pat, base, cm, allow_small_or_imprecise_dtypes=True), "", w)

    def scan(out, d0, d1, op0, op1, r, w):
        do("V", lambda v: v.tensor_tensor_scan(out, d0, d1, 0.0, op0, op1), r, w)

    dma("S", "ncl", T.NL[:, :], T.ncl[:, :], "", "NL")
    dma("S", "lim", T.LM[:, :], T.lim[:, :], "", "LM")
    dma("A", "rb0", T.RB[:, 0:256], T.rb[:, 0:256], "", "RB0")
    dma("A", "ra0", T.RA[:, 0:256], T.ra[:, 0:256], "", "RA0")
    dma("A", "rc0", T.RC[:, 0:256], T.rc[:, 0:256], "", "RC0")
    dma("S", "bank", T.bankS[:, 0:B], T.bank[:, :], "", "bk")
    iota(T.PID[:, :], [[1, 1]], 1, "PID")
    iota(T.IG[:, :], [[1, 8], [0, 16]], 0, "IG")
    iota(T.II[:, :], [[0, 8], [1, 16]], 0, "II")
    iota(T.IR[:, :], [[1, 256]], 0, "IR")
    ms(T.ONE[:, :], 1.0, "ONE")
    for n in ("b", "a", "c"):
        dma("S", "r%s1" % n, T["R" + n.upper()][:, 256:1024], T["r" + n][:, 256:1024], "", "R%s1" % n.upper())
    do("G", lambda q: q.affine_select(T.DG[:, :], T.ONE[:, 0:128], [[1, 128]], ALU.is_equal, 0.0, 0, -1), "ONE", "DG")
    iota(T.bankS[:, B:4096], [[0, 1024]], 0, "bkz")
    iota(T.GB[:, :], [[1, 8], [0, 32]], 0, "GB")
    do("G", lambda q: q.affine_select(T.TRI[:, :], T.ONE[:, 0:128], [[1, 128]], ALU.is_gt, 0.0, 0, -1), "ONE", "TRI")
    do("G", lambda q: q.affine_select(T.BID[:, :], T.DG[:, :], [[1, 128]], ALU.not_equal, -1.0, -1, -1), "DG", "BID")
    iota(T.IF[:, :], [[0, 16], [1, 16]], 0, "IF")
    iota(T.I9[:, :], [[0, 16], [1, 9]], 0, "I9")
    iota(T.I16[:, :, :], [[0, 16], [1, 16]], 0, "I16")
    iota(T.JL[:, :], [[16, 16]], 0, "JL")
    iota(T.LI[:, :], [[0, 2048]], 0, "LI")
    iota(T.LP[:, :], [[0, 2048]], 0, "LP")
    iota(T.USED[:, 0:4096], [[0, 4096]], 0, "USED")
    iota(T.USED[:, 4096:4112], [[0, 16]], 0, "USEDx", 1)
    iota(T.ONEI[:, :], [[0, 256]], 0, "ONEI", 1)
    dma("S", "used", T.USED[0:128:16, 0:4096], T.used[:, :], "", "USED")

    CC = T.CC
    col = {n: CC[:, k:k + 1] for k, n in enumerate(
        ["pid", "i", "m", "typ", "grp", "p8", "c16", "wt", "podd", "sgs", "msg", "off", "tm1", "cval", "i0",
         "mm1", "sm0", "sm1", "sm2", "sm3", "t0", "t1", "c32", "m15", "on1"])}
    for k, (sh, an) in enumerate([(0, 255), (0, 15), (1, 7), (0, 1), (4, 7), (0, 7), (3, 15)]):
        ts(T.TI[:, k:k + 1], T.PID[:, :], sh, ALU.arith_shift_right, "PID", "TI%d" % k, an, ALU.bitwise_and)
    cp(CC[:, 0:7], T.TI[:, 0:7], "TI0 TI1 TI2 TI3 TI4 TI5 TI6", "CC")
    for n, src, a, b, key in (("tm1", "typ", 1.0 / 256, -1.0 / 256, "CCt"), ("sm0", "m", -1.0, 3.0, "CCx0"), ("mm1", "m", 1.0, -1.0, "CCn"), ("msg", "typ", -2.0, 1.0, "CCm"),
                              ("off", "typ", -1.0, 1.0, "CCf"), ("wt", "i", 14.0, 9.0, "CCw"), ("sm1", "m", -1.0, 4.0, "CCx1"), ("sm2", "m", -1.0, 5.0, "CCx2"),
                              ("sm3", "m", -1.0, 6.0, "CCx3"), ("podd", "p8", 2.0, 1.0, "CCo"), ("c32", "c16", 1.0, 16.0, "CC2"),
                              ("m15", "pid", 0.0, -15.0, "CCg"), ("on1", "pid", 0.0, 1.0, "CCh")):
        act(col[n], col[src], AF.Copy, "CC", key, a, b)
        if n == "mm1":
            act(T.COLT[:, :], T.IR[:, :], AF.Identity, "IR CCt", "COLT", 1.0 / 256, col["tm1"])
    act(T.JC[:, :], col["pid"], AF.Copy, "CC", "JC")
    ts(col["sgs"], col["typ"], 2.0 / 4096, ALU.mult, "CC", "CCs", -1.0 / 4096, ALU.add)
    ts(T.BON[:, :], T.IG[:, :], col["grp"], ALU.is_equal, "IG CC", "BON")
    ts(T.SL8[:, :], T.IG[0:8, :], CC[0:8, 0:1], ALU.is_equal, "IG CC", "SL8")
    ts(T.IT[:, :], T.II[:, :], col["sgs"], ALU.mult, "II CCs", "IT", 9999.0 / 4096, ALU.add)
    ts(T.MK[:, :], T.IR[:, 0:8], col["m"], ALU.is_equal, "IR CC", "MK")
    ts(col["i0"], col["i"], 0.0, ALU.is_equal, "CC", "CCi")
    tt(T.IT[:, :], T.IT[:, :], T.BON[:, :], ALU.mult, "IT BON", "IT")
    ts(T.MS[:, :], T.IR[:, 0:8], col["mm1"], ALU.is_equal, "IR CCn", "MS")
    ms(T.RQ[:, :], 1.0, "RQ")
    ts(T.IT[:, :], T.IT[:, :], -9999.0 / 4096, ALU.add, "IT", "IT")
    ms(T.RQ[:, 0:32:8], 0.0, "RQ")
    tt(T.MD[:, :], T.MK[:, :], T.MS[:, :], ALU.subtract, "MK MS", "MD")
    cp(T.NLF[:, :], T.NL[:, :], "NL", "NLF")
    for b in ("b0", "b7"):
        mm(T[b][:, 0:4], T.SL8[:, :], T.NLF[:, :], "SL8 NLF", b)

    def masks(t):
        q, s = 32 * t, 4 + t
        ts(T.PR[:, :], T.IR[:, 0:8], col["sm%d" % t], ALU.is_equal, "IR CCx%d" % t, "PR")
        ts(T.DS[:, 0:8], T.IR[:, 0:8], 1.0, ALU.subtract, "IR CCx%d" % t, "DS", col["sm%d" % t], ALU.is_equal)
        ts(T.DS[:, 24:32], T.IR[:, 0:8], float(s - 1), ALU.is_le, "IR", "DSd")
        ts(T.MQ[:, q:q + 8], T.MD[:, :], 1.0 / 4096, ALU.mult, "MD", "MQ%d" % t)
        tt(T.DS[:, 8:16], T.PR[:, :], T.DS[:, 0:8], ALU.subtract, "PR DS", "DSb")
        ts(T.DQ[:, 0:8], T.DS[:, 24:32], T.MK[:, 0:1], ALU.mult, "DSd MK", "DQ")
        cp(T.MQ[:, q + 16:q + 24], T.MS[:, :], "MS", "MQ%da" % t)
        ts(T.MQ[:, q + 8:q + 16], T.DS[:, 8:16], 1.0 / 4096, ALU.mult, "DSb", "MQ%db" % t)
        tt(T.MQ[:, q + 24:q + 32], T.DQ[:, 0:8], T.PR[:, :], ALU.subtract, "DQ PR", "MQ%dc" % t)
    masks(0)
    ms(T.F4[:, :], 0.0, "F4")
    ms(T.R8[:, :], 0.0, "R8")
    ms(T.SEL[:, :], 0.0, "SEL")
    for k in range(4):
        cp(T.F4[:, 8 * k:8 * k + 4], T.b0[:, 0:4], "b0 F4", "F4%d" % k)
        act(T.R8[:, 7 - k:8 - k], T.b7[:, k:k + 1], AF.Copy, "b7 R8", "R8%d" % k)
    ms(T.NEGM[:, :], -M4096, "NEGM")
    ts(col["t0"], col["i"], 1.0, ALU.is_equal, "CC", "CC0", 2.0 ** -13, ALU.mult)
    ts(col["t1"], col["i"], 2.0, ALU.is_equal, "CC", "CC1", -float(MID), ALU.mult)
    ms(T.TC[:, 0:1], float(B), "TC")
    ts(col["cval"], col["i0"], -0.5, ALU.mult, "CCi CC0", "CCv", col["t0"], ALU.add)
    ms(T.TC[:, 1:2], B / 4096.0, "TC1")
    tt(col["cval"], col["cval"], col["t1"], ALU.add, "CCv CC1", "CCv")

    bankk = "bk bkz"
    win = T.bankS[:, 0:4096]
    c0 = -(MID + 0.5) + 2.0 ** -13
    F4k, R8k = "F4 F40 F41 F42 F43", "R8 R80 R81 R82 R83"

    def prep(t, app=()):
        app = list(app) + [lambda: None] * (5 - len(app))
        s = 4 + t
        CS, SEL = T.CS, T.SEL
        ct = SEL[:, s:s + 1]
        c = slice(256 * t, 256 * t + 256)
        tt(T.DQ[:, :], T.F4[:, :], T.MQ[:, 32 * t:32 * t + 32], ALU.mult, F4k + " MQ%d MQ%da MQ%db MQ%dc" % (t, t, t, t), "DQ")
        tt(T.PP[:, 0:s], T.F4[:, 0:s], T.R8[:, 8 - s:8], ALU.mult, F4k + " " + R8k, "PP")
        scan(T.DS[:, :], T.RQ[:, :], T.DQ[:, :], ALU.mult, ALU.add, "RQ DQ", "DS")
        ts(T.PR[:, 0:s], T.PP[:, 0:s], -2047.5, ALU.add, "PP", "PR", M4096, ALU.add)
        scan(SEL[:, 1:s + 1], T.PR[:, 0:s], T.NEGM[:, 0:s], ALU.add, ALU.add, "PR NEGM", "SEL")
        ts(T.HI[:, 0:2], T.DS[:, 7:16:8], MN, ALU.add, "DS", "HI", MN, ALU.subtract)
        tt(T.SM[:, :], SEL[:, 0:8], T.MK[:, :], ALU.mult, "SEL MK", "SM")
        do("V", lambda v: v.reciprocal(CS[:, 1:2], ct), "SEL", "CS1")
        do("V", lambda v: v.tensor_reduce(CS[:, 2:3], T.SM[:, :], AX.X, ALU.add), "SM", "CS2")
        ts(T.HI[:, 2:4], T.DS[:, 23:32:8], M32, ALU.add, "DS", "HI2", M32, ALU.subtract)
        app[0]()
        ts(CS[:, 3:4], CS[:, 2:3], CS[:, 1:2], ALU.mult, "CS1 CS2", "CS3", -0.46875 / 256, ALU.add)
        app[1]()
        tt(T.LO[:, :], T.DS[:, 7:32:8], T.HI[:, :], ALU.subtract, "DS HI HI2", "LO")
        ts(CS[:, 4:5], CS[:, 3:4], M256, ALU.add, "CS3", "CS4", M256, ALU.subtract)
        if t:
            act(T.Z1[:, :], T.RCF[:, c], AF.Copy, "RCF TC1", "Z1", T.TC[:, 1:2], c0)
        else:
            ts(T.Z1[:, :], T.RC[:, c], T.TC[:, 1:2], ALU.mult, "RC0 TC1", "Z1", c0, ALU.add)
        app[2]()
        ts(CS[:, 5:6], CS[:, 4:5], ct, ALU.mult, "SEL CS2 CS4", "CS5", CS[:, 2:3], ALU.subtract)
        app[3]()
        ts(T.OZ[:, :], T.Z1[:, :], M1, ALU.add, "Z1", "OZ", M1 - MID, ALU.subtract)
        ts(CS[:, 6:7], CS[:, 5:6], col["msg"], ALU.mult, "CS5 CCm CCf", "CS6", col["off"], ALU.add)
        app[4]()

    def lists(t):
        CS, ct, k = T.CS, T.SEL[:, 4 + t:5 + t], "%d" % (t > 0)
        c = slice(256 * t, 256 * t + 256)
        ts(T.RH[:, :], T.COLT[:, :], CS[:, 4:5], ALU.is_ge, "COLT CS4", "RH")
        ts(T.IND[:, :], T.IT[:, :], ct, ALU.mult, "IT SEL CS6", "IND", CS[:, 6:7], ALU.is_ge)
        for b in ("b2", "b4"):
            mm(T[b][:, 0:256], T.CL[:, :], T.ONE[:, :], "CL ONE", b, True, False)
        for q, b in ((1, "b1"), (3, "b2"), (0, "b3"), (2, "b4")):
            for h in (0, 1):
                n = 2 * q + h
                if h == 0:
                    ts(T.LQ[:, 128 * n:128 * n + 128], T.IND[:, :], T.HI[:, q:q + 1], ALU.mult, "IND HI HI2", "LQ%d" % n)
                else:
                    act(T.LQ[:, 128 * n:128 * n + 128], T.IND[:, :], AF.Copy, "IND LO", "LQ%d" % n, T.LO[:, q:q + 1])
                mm(T[b][:, 0:256], T.LQ[:, 128 * n:128 * n + 128], T.RH[:, :], "LQ%d RH" % n, b, q < 2 and h == 0, h == 1)
        act(T.ZG[:, :], win.indirect(T.OZ[:, 192:224]), AF.Copy, "OZ " + bankk, "ZG")
        for w, r, o, bn, bs in (("V1", "RB", "OY", "b1", "b2"), ("W1", "RA", "OX", "b3", "b4")):
            tt(T[w][:, :], T[bn][:, 0:256], T[r][:, c], ALU.mult, bn + " " + r + k, w)
            tt(T[w][:, :], T[w][:, :], T[bs][:, 0:256], ALU.add, w + " " + bs, w)
            ts(T[o][:, :], T[w][:, :], M1, ALU.add, w, o, M1 - MID, ALU.subtract)

    def build(t, h0, h1):
        def y(q, dst="YG", lst="OY", a=0, n=1024):
            o = 1024 * q + a
            act(T[dst][:, o:o + n], win.indirect(T[lst][:, o // 16:(o + n) // 16]), AF.Copy, lst + " " + bankk, "%s%d%d" % (dst, q, a))

        def x(q, a=0, n=1024):
            o = slice(1024 * q + a, 1024 * q + a + n)
            tt(T.FX[:, o], win.indirect(T.OX[:, 64 * q + a // 16:64 * q + (a + n) // 16]), T.YG[:, o], (ALU.min, ALU.max, None, ALU.add)[q], "OX YG%d%d " % (q, a) + bankk, "FX%d%d" % (q, a))

        def both(q, b, o, lh):
            k = (q, o - 1024 * q)
            mm(T[b][:, :], T.DG[:, :], T.XG[:, o:o + 512], "DG XG%d%d" % k, b, True, False)
            mm(T[b][:, :], T[lh][:, :], T.YG[:, o:o + 512], lh + " YG%d%d" % k, b, False, True)

        def z(q, a=0, n=1024):
            o = 1024 * q + a
            tt(T.K[:, o:o + n], win.indirect(T.OZ[:, o // 16:(o + n) // 16]), T.FX[:, o:o + n], ALU.min, "OZ FX%d%d FX%d512 " % (q, a, q) + bankk, "K%d%d" % (q, a))

        def sums(q, n=1024):
            for b in range(32):
                mm(T.b0[32 * q:32 * q + n // 32, b:512:32], T.K[:, 1024 * q + b:1024 * q + n:32], T.WCP[:, :], "WCP K%d0 K%d512" % (q, q), "b0")
        y(0, n=512)
        y(0, a=512, n=512)
        y(1)
        x(0, 0, 512)
        x(0, 512, 512)
        h0()
        h1()
        z(0)
        sums(0)
        for a, b in ((0, "b5"), (512, "b6")):
            y(2, a=a, n=512)
            y(2, "XG", "OX", a=a, n=512)
            both(2, b, 2048 + a, "NDG")
        x(1)
        z(1)
        y(3, a=512, n=512)
        act(T.FX[:, 2048:2560], T.b5[:, :], AF.Abs, "b5", "FX20")
        act(T.FX[:, 2560:3072], T.b6[:, :], AF.Abs, "b6", "FX2512")
        sums(1)
        x(3, 512, 512)
        z(3, 512, 512)
        if t:
            sums(3)
        y(3, n=512)
        y(3, "XG", "OX", n=512)
        both(3, "b7", 3072, "DG")
        z(2)
        sums(2)
        tt(T.K[:, 3072:3584], T.b7[:, :], T.ZG[:, :], ALU.min, "b7 ZG", "K30")
        sums(3, 512 if t else 1024)

    def pick(t, h):
        tt(T.Z1[:, :], T.b0[:, 0:256], T.MIDT[:, :], ALU.subtract, "b0 MIDT", "Z1")
        act(T.b7[:, 0:256], T.Z1[:, :], AF.Abs, "Z1", "b7")
        ts(T.OI[:, :], T.b0[:, 256:512], 2.0, ALU.mult, "b0", "OI", 1.0, ALU.add)
        ts(T.OJ[:, :], T.OI[:, :], 15, ALU.bitwise_and, "OI", "OJ")
        tt(T.b7[:, 256:512], T.b7[:, 0:256], T.HALF[:, :], ALU.is_le, "b7 HALF", "b7")
        tt(T.OWN[:, :], T.OJ[:, :], T.b7[:, 256:512], ALU.mult, "OJ b7", "OWN")
        act(T.OA[:, :], T.OWN[:, :], AF.Abs, "OWN CCg", "OA", 1.0, col["m15"])
        act(T.O[:, 1792:2048], T.OA[:, :], AF.Relu, "OA CCh", "O7", -1.0, col["on1"])
        for p in range(7):
            ts(T.O[:, 256 * p:256 * p + 256], T.OWN[:, :], 2.0 * p + 1, ALU.is_equal, "OWN", "O%d" % p)
        h()
        for q in range(8):
            mm(T.b6[:, SEG * q + 9:SEG * q + SEG], T.BID[:, :], T.OWN[:, 32 * q:32 * q + 32], "BID OWN", "b6")
            mm(T.b6[:, SEG * q + 8:SEG * q + 9], T.BID[:, :], T.JC[:, :], "BID JC", "b6")
        for b in range(32):
            mm(T.b5[:, 0:64], T.TRI[:, :], T.O[:, b:2048:32], "TRI O0 O1 O2 O3 O4 O5 O6 O7", "b5", b == 0, b == 31)
        for r in range(4):
            ts(T.S4[:, 64 * r:64 * r + 64], T.b5[:, 0:64], -float(r), ALU.add, "b5", "S4%d" % r, 100.0, ALU.min)
        for q in range(8):
            mm(T.b6[:, SEG * q:SEG * q + 8], T.BID[:, :], T.S4[:, q:64:8], "BID S40", "b6")
        act(T.Z[:, :], T.b6[:, 0:8 * SEG], AF.Copy, "b6", "Z")
        for c in range(8):
            ts(T.U[:, 256 * c:256 * c + 256], T.S4[:, :], 4.0 * c, ALU.is_le, "S40 S41 S42 S43", "U%d" % c)
        for ch in (0, 1):
            for lo, hi, b in ((0, 9, "b%d" % (3 + ch)), (9, SEG, "b%d" % (1 + ch))):
                for q in range(8):
                    mm(T[b][:, (hi - lo) * q:(hi - lo) * (q + 1)], T.U[:, 1024 * ch + q:1024 * ch + 1024:8], T.Z[:, SEG * q + lo:SEG * q + hi],
                       "Z U%d U%d U%d U%d" % tuple(range(4 * ch, 4 * ch + 4)), b)
        for ch in (0, 1):
            d, b = slice(72 * ch, 72 * ch + 72), T["b%d" % (3 + ch)]
            tt(T.SMM[:, d], b[:, 0:72], T.MSK[:, d], ALU.mult, "b%d MSK" % (3 + ch), "SMM%d" % ch)
            act(T.R32[:, 8 * ch:8 * ch + 8], b[:, 8:72:9], AF.Copy, "b%d" % (3 + ch), "R32%d" % ch, 32.0, -2048.0)
            if ch:
                scan(T.SS[:, :], T.RSS[:, :], T.SMM[:, :], ALU.mult, ALU.add, "RSS SMM0 SMM1", "SS")
            ts(T.EO[:, 256 * ch:256 * ch + 256], T["b%d" % (1 + ch)][:, 0:256], col["podd"], ALU.is_equal, "b%d CCo" % (1 + ch), "EO%d" % ch)
        tt(T.EO[:, 0:512:32], T.EO[:, 0:512:32], T.SS[:, 8:144:9], ALU.add, "SS EO0 EO1", "EO0 EO1")
        scan(T.CU[:, :], T.RS[:, :], T.EO[:, :], ALU.mult, ALU.add, "RS EO0 EO1", "CU")
        ts(T.IN[:, 0:256], T.CU[:, 0:256], col["c16"], ALU.is_le, "CU CC", "IN0")
        ts(T.IN[:, 256:512], T.CU[:, 256:512], col["c32"], ALU.is_le, "CU CC2", "IN1")
        scan(T.C2[:, :], T.RS[:, :], T.IN[:, :], ALU.mult, ALU.add, "RS IN0 IN1", "C2")
        tt(T.J16[:, :], T.C2[:, 31:512:32], T.R32[:, :], ALU.add, "C2 R320 R321", "J16")
        do("V", lambda v: v.tensor_tensor(T.LJ[:, :], T.J16[:, :].indirect(T.OC[:, :]), T.MI[:, :], ALU.mult), "J16 OC MI", "LJ")
        for ch in (0, 1):
            mm(T.b5[:, ch:16:2], T.LJ[:, 128 * ch:128 * ch + 128], T.RP[:, :], "LJ RP", "b5")
        ts(T.OFJ[:, :], T.b5[:, 0:16], 2048.0, ALU.add, "b5", "OFJ")
        o = 256 * t
        do("V", lambda v: v.tensor_copy(T.send[:, o:o + 256], T.K[:, 0:4112].indirect(T.OFJ[:, :])), "OFJ K00 K10 K20 K30 K3512 kinv", "snd%d" % t)
        tr, k = [], 0
        for p in range(NR):
            if p == rank:
                continue
            dst = T.cores[p]
            e = topo.engines(core, dst)
            rid, pid, _se = topo.addr(dst)
            tr.append(RemoteDMATransfer(dst_ids=[DstId(rid=rid, pnc=pid)], dma_engine_mask=(1 << e[2 * k]) | (1 << e[2 * k + 1]), remote_sem=T.sem["arr%d" % t],
                                        srcs=[T.send[:, o + 32 * p:o + 32 * p + 32]], dsts=[T.land[:, o + 32 * rank:o + 32 * rank + 32]]))
            k += 1
        order("G", ["snd%d" % t], [])
        g.remote_dma_fused(tr, local_sem=T.sem["sent%d" % t])
        cp(T.land[:, o + 32 * rank:o + 32 * rank + 32], T.send[:, o + 32 * rank:o + 32 * rank + 32], "snd%d" % t, "lnd%d" % t)

    def keep(t):
        s, last = 4 + t, t == RO - 1
        o, lk = 256 * t, "lnd%d" % t
        lnd = T.land[:, o:o + 256]
        ts(T.TC[:, 3:4], T.TC[:, 0:1], -1.0, ALU.add, "TC", "TB")
        ts(T.WJ[:, :], T.JL[:, :], T.TC[:, 0:1], ALU.subtract, "JLx TC", "WJ", 4097.0, ALU.add)
        wait("P", "arr%d" % t, 14)
        mm(T.b3[:, 0:256], T.WBL[:, :], lnd, "WBL " + lk, "b3")
        for i in range(16):
            mm(T.b4[:, 0:16], T.LI[:, 128 * i:128 * i + 128], T.land[:, o + i:o + 256:16], "LI LI%d " % i + lk, "b4", i == 0, i == 15)
        cp(T.OI[:, :], T.b3[:, 0:256], "b3", "OI")
        ts(T.OJ[:, :], T.OI[:, :], 3, ALU.arith_shift_right, "OI", "OJ", 4095, ALU.bitwise_and)
        cp(T.KLI[:, :], T.b4[:, 0:16], "b4", "KLI")
        ts(T.KBH[:, :], T.OJ[:, :], -2048.0, ALU.add, "OJ", "KBH")
        ts(T.KLJ[:, :], T.KLI[:, :], 3, ALU.arith_shift_right, "KLI", "KLJ", 4095, ALU.bitwise_and)
        ts(T.INV[:, :], T.b4[:, 0:16], 0.0, ALU.is_lt, "b4", "INV", 4096.0, ALU.mult)
        tt(T.BL[:, :], T.KLJ[:, :], T.INV[:, :], ALU.max, "KLJ INV", "BL")

        def ed(a, b):
            return " ".join("Ed%d" % m for m in range(a, b))

        def later(a, b):
            tt(T.E3[:, a:b, 0:16], T.E3[:, a:b, 0:16], T.DM[:, a:b, :], ALU.mult, ed(a, b) + " DM", ed(a, b))
        for m in range(16):
            ts(T.E3[:, m, 0:256 - 16 * m], T.KBH[:, 16 * m:256], 2048.0, ALU.add, "KBH BL", "E%d Ed%d" % (m, m), T.BL[:, m:m + 1], ALU.is_equal)
            if m == 0:
                cp(T.BU[:, :], T.BL[:, :], "BL", "BU")
            if m == 1:
                do("V", lambda v: v.tensor_copy(T.UG[:, :], T.USED[:, 0:4112].indirect(T.BU[:, :])), "USED USEDx BU", "UG")
                mm(T.b6[:, 0:256], T.W0[:, :], T.UG[:, :], "W0 UG", "b6", True, False)
            if m == NA + 1:
                later(0, NA)
        later(NA, 16)
        for m in range(15):
            mm(T.b6[:, 16 * m + 16:256], T.BON[:, :], T.E3[:, m, 16:256 - 16 * m], "BON E%d" % m, "b6", False, False)
        mm(T.b6[:, 0:256], T.BON[:, :], T.E3[:, :, 0:16], "BON " + ed(0, 16), "b6", False, True)
        ts(T.b7[:, 0:256], T.b6[:, 0:256], 0.5, ALU.is_lt, "b6", "b7")
        scan(T.POS[:, :], T.ZERO[:, :], T.b7[:, 0:256], ALU.max, ALU.add, "ZERO b7", "POS")
        n = T.POS[:, 255:256]
        if not last:
            tt(T.TC[:, 0:1], T.TC[:, 0:1], n, ALU.add, "TC POS", "TC")
            ts(T.F4[:, s:32:8], T.ONEF[:, 0:4], n, ALU.mult, "ONEF POS", "F4")
            cp(T.R8[:, 7 - s:8 - s], n, "POS", "R8")
        tt(T.X[:, :], T.b7[:, 0:256], T.POS[:, :], ALU.mult, "b7 POS", "X")
        if not last:
            ts(T.TC[:, 1:2], T.TC[:, 0:1], 1.0 / 4096, ALU.mult, "TC", "TC1")
        for i in range(16):
            mm(T.b5[:, 0:16], T.LP[:, 128 * i:128 * i + 128], T.X[:, i:256:16], "LP LP%d X" % i, "b5", i == 0, i == 15)
        app = (lambda: ts(T.ZT[:, :], T.b5[:, 0:16], 0.0, ALU.is_equal, "b5", "ZT"),
               lambda: tt(T.D1[:, :], T.ZT[:, :], T.WJ[:, :], ALU.mult, "ZT WJ", "D1"),
               lambda: tt(T.D1[:, :], T.D1[:, :], T.b5[:, 0:16], ALU.add, "D1 b5", "D1"),
               lambda: ts(T.DU[:, :], T.D1[:, :], T.TC[:, 3:4], ALU.add, "D1 TB", "DU"),
               lambda: do("V", lambda v: v.tensor_copy(T.bankS[:, 0:4352].indirect(T.DU[:, :]), lnd), lk + " DU", "bk bkz"))
        if last:
            for f in app:
                f()
        else:
            prep(t + 1, app)

    def mark(t):
        tt(T.UJ[:, :], T.JL[:, :], T.BL[:, :], ALU.subtract, "JLx BL", "UJ")
        ts(T.E1[:, :], T.UJ[:, :], 4112.0, ALU.add, "UJ", "E1")
        tt(T.E1[:, :], T.E1[:, :], T.ZT[:, :], ALU.mult, "E1 ZT", "E1")
        tt(T.E1[:, :], T.E1[:, :], T.BL[:, :], ALU.add, "E1 BL", "E1")
        cp(T.EU[:, :], T.E1[:, :], "E1", "EU")
        do("V", lambda v: v.tensor_copy(T.USED[:, 0:4368].indirect(T.EU[:, :]), T.ONEI[:, :]), "EU ONEI", "USED USEDx")

    prep(0)
    ts(T.CL[:, :], T.BON[:, :], col["cval"], ALU.mult, "BON CCv", "CL")
    lists(0)

    def h0():
        cp(T.LMF[:, 0:2], T.LM[:, :], "LM", "LMF")
        ms(T.ONEF[:, :], 1.0, "ONEF")
        tt(T.LMF[:, 2:3], T.LMF[:, 0:1], T.LMF[:, 1:2], ALU.add, "LMF", "LMF2")
        tt(T.LMF[:, 3:4], T.LMF[:, 1:2], T.LMF[:, 0:1], ALU.subtract, "LMF", "LMF3")
        ts(T.NDG[:, :], T.DG[:, :], -1.0, ALU.mult, "DG", "NDG")
        ts(T.LMF[:, 4:6], T.LMF[:, 2:4], 0.5, ALU.mult, "LMF2 LMF3", "LMF4")

    def h1():
        ts(T.WCP[:, 0:8], T.IR[:, 0:8], col["grp"], ALU.is_equal, "IR CC", "WCPa")
        ts(T.WCP[:, 8:16], T.IR[:, 0:8], col["grp"], ALU.is_equal, "IR CC CCw WCPa", "WCP", col["wt"], ALU.mult)
        for h in (0, 1):
            ts(T.DM8[:, 256 * h:256 * h + 256], T.GB[0:8, :], CC[0:8, 0:1], ALU.is_equal, "GB CC LMF4", "DM8%d" % h, T.LMF[:, 4 + h:5 + h], ALU.mult)

    def h2():
        ms(T.RS[:, :], 1.0, "RS")
        ms(T.RSS[:, :], 1.0, "RSS")
        ms(T.ZERO[:, :], 0.0, "ZERO")
        ms(T.RS[:, 0:512:32], 0.0, "RS")
        ms(T.RSS[:, 0:144:9], 0.0, "RSS")
        ms(T.K[:, 4096:4112], -32.0, "kinv")
        cp(T.OC[:, :], T.IR[:, 0:16], "IR", "OC")
        ts(T.MSK[:, :], T.I9[:, :], col["p8"], ALU.is_equal, "I9 CC", "MSK")
        ts(T.MI[:, :], T.IF[:, :], col["c16"], ALU.is_equal, "IF CC", "MI")
        ts(T.RP[:, :], T.IR[:, 0:8], col["p8"], ALU.is_equal, "IR CC", "RP")
        ts(T.W0C[:, :], T.IR[:, 0:8], col["grp"], ALU.is_equal, "IR CC CCi", "W0C", col["i0"], ALU.mult)
    build(0, h0, h1)
    mm(T.b1[:, :], T.ONEF[0:8, :], T.DM8[:, :], "ONEF DM80 DM81", "b1")
    act(T.MIDT[:, :], T.b1[:, 0:256], AF.Copy, "b1", "MIDT")
    act(T.HALF[:, :], T.b1[:, 256:512], AF.Copy, "b1", "HALF")
    pick(0, h2)
    for i in range(16):
        act(T.LI[:, 129 * i:128 * i + 128:16], T.WCP[:, 8:16], AF.Copy, "WCP LI", "LI%d" % i)
    for i in range(16):
        act(T.LP[:, 129 * i:128 * i + 128:16], T.W0C[:, :], AF.Copy, "W0C LP", "LP%d" % i)
    ts(T.WBL[:, :], T.IG[:, :], col["grp"], ALU.is_equal, "IG CC CCw", "WBL", col["wt"], ALU.mult)
    ts(T.W0[:, :], T.BON[:, :], col["i0"], ALU.mult, "BON CCi", "W0")
    ts(T.DM[:, :, :], T.I16[:, :, :], col["i"], ALU.is_gt, "I16 CC", "DM")
    ts(T.JL[:, :], T.JL[:, :], col["i"], ALU.add, "JL CC", "JLx")
    masks(1)
    cp(T.RCF[:, 256:1024], T.RC[:, 256:1024], "RC1", "RCF")
    keep(0)
    for t in range(1, RO):
        lists(t)
        build(t, lambda: None, lambda: None)
        pick(t, lambda: masks(t + 1) if t + 1 < RO else None)
        mark(t - 1)
        keep(t)
    dma("S", "out", T.y[:, :], T.bankS[:, B:4096], "bk bkz", "out")
    for t in range(RO):
        g.wait_ge(T.sem["sent%d" % t], 14)
    for e in ("V", "A", "P", "G"):
        g.wait_ge(T.sem["s" + e], cnt[e])
    for n in _DMAS:
        g.wait_ge(T.sem["d_" + n], 16)
